import numpy as np
import ml_dtypes


def mxq(x, axis, fmt="e4m3"):
    dtype, down = {"e4m3": (ml_dtypes.float8_e4m3fn, 7), "e5m2": (ml_dtypes.float8_e5m2, 14)}[fmt]
    v = np.moveaxis(np.asarray(x, np.float32).astype(ml_dtypes.bfloat16).astype(np.float64), axis, -1)
    blocks = v.reshape(v.shape[:-1] + (-1, 32))
    amax = np.abs(blocks).max(-1, keepdims=True)
    byte = np.maximum(np.where(amax > 0, np.frexp(amax)[1] - 1 + 127, 0) - down, 1)
    scale = np.exp2(byte - 127.0)
    codes = (blocks / scale).astype(np.float32).astype(dtype).astype(np.float64)
    return np.moveaxis((codes * scale).reshape(v.shape), -1, axis)


WIDE = False


def mx_kscale(k):
    if not WIDE:
        return np.ones(k)
    levels = np.array([10, -10, 5, -5, 0])
    if k % 512:
        return np.exp2(np.random.permutation(np.resize(levels, k // 32))).repeat(32)
    a = np.empty((k // 512, 16))
    for p in range(k // 512):
        a[p, :8] = np.random.permutation(np.resize(levels, 8))
        for g in range(8):
            far = levels[np.abs(levels - a[p, g]) >= 10]
            a[p, g + 8] = far[np.random.randint(len(far))]
    return np.exp2(a.ravel()).repeat(32)


def f64(x):
    return np.asarray(x).astype(np.float64)


def striped(idx):
    return np.tile(idx.reshape(-1, 16).T, (8, 1)).astype(np.uint16)


def unstriped(offs):
    return offs[:16].T.reshape(-1).astype(np.int64)


E2M1 = np.array([0.0, 0.5, 1.0, 1.5, 2.0, 3.0, 4.0, 6.0, -0.0, -0.5, -1.0, -1.5, -2.0, -3.0, -4.0, -6.0])


def pack_weight(w, fmt):
    k, n = w.shape
    w = f64(np.asarray(w, np.float32).astype(ml_dtypes.bfloat16)).reshape(k // 32, 32, n)
    amax = np.abs(w).max(1)
    if fmt == "e4m3":
        byte = np.frexp(amax)[1] - 1 + 127 - 7
    else:
        mant, ex = np.frexp(amax / 6.0)
        byte = np.where(mant > 0.5, ex, ex - 1) + 127
    byte = np.clip(np.where(amax > 0, byte, 1), 1, 254)
    scaled = (w * np.exp2(127.0 - byte)[:, None, :]).reshape(k, n).astype(np.float32)
    by_word = np.ascontiguousarray(scaled.reshape(k // 512, 128, 4, n).transpose(0, 1, 3, 2))
    if fmt == "e4m3":
        words = by_word.astype(ml_dtypes.float8_e4m3fn).view(np.uint8)
    else:
        c = by_word.astype(ml_dtypes.float4_e2m1fn).view(np.uint8) & 0xF
        words = (c[..., 0::2] | (c[..., 1::2] << 4)).reshape(k // 512, 128, 2 * n)
    return np.ascontiguousarray(words), np.ascontiguousarray(byte.astype(np.uint8).reshape(k // 512, 16, n))


def unpack_weight(words, scales, fmt):
    g, _, n = scales.shape
    words = np.ascontiguousarray(words).reshape(g, 128, n, -1)
    if fmt == "e4m3":
        vals = words.view(ml_dtypes.float8_e4m3fn).astype(np.float64)
    else:
        nib = np.empty((g, 128, n, 4), np.uint8)
        nib[..., 0::2] = words & 0xF
        nib[..., 1::2] = words >> 4
        vals = E2M1[nib]
    vals = vals * np.repeat(np.exp2(scales.astype(np.float64) - 127.0), 8, axis=1)[..., None]
    return vals.transpose(0, 1, 3, 2).reshape(g * 512, n)


def gelu(v):
    return 0.5 * v * (1.0 + np.tanh(np.sqrt(2.0 / np.pi) * (v + 0.044715 * v**3)))


K, K1, K2, H, T, S, T2, P = 2048, 1024, 1024, 1024, 2048, 512, 1024, 512

def setup_inputs():
    n = np.random.standard_normal
    s = mx_kscale(K)[:, None]
    u = mx_kscale(H)[:, None]
    d = {}
    d["tab_words"], d["tab_scales"] = pack_weight(n((K, T)) * s, "e4m3")
    d["offs"] = striped(np.random.permutation(T)[:S])
    d["w1"] = (1.5 * n((K1, H)) / K ** 0.5 / s[:K1]).astype(np.float32)
    d["w4_words"], d["w4_scales"] = pack_weight(1.5 * n((K2, H)) / K ** 0.5 / s[K1:], "e2m1")
    d["gain"] = (1.3 * np.exp(0.3 * n(H)) * u[:, 0]).astype(np.float32)
    d["page0"] = (n((H, T2)) * u).astype(np.float32)
    d["wgs"] = np.exp(0.3 * n((128, S))).astype(np.float32)
    d["offs2"] = striped(np.random.permutation(T2)[:S])
    d["offs3"] = striped(np.random.permutation(T2)[:P])
    d["rv"] = (n(H) / H ** 0.5 / u[:, 0] ** 2).astype(np.float32)
    d["slot"] = n(T2).astype(np.float32)
    return d

def reference(tab_words, tab_scales, offs, w1, w4_words, w4_scales, gain, page0, wgs, offs2, offs3, rv, slot):
    v = unpack_weight(tab_words, tab_scales, "e4m3")[:, unstriped(offs)]
    w1q = mxq(f64(w1), 0, "e4m3")
    w4 = unpack_weight(w4_words, w4_scales, "e2m1")
    f = w1q.T @ v[:K1] + w4.T @ v[K1:]
    h = f64(gain)[:, None] * np.tanh(f)
    page = f64(page0).copy()
    page[:, unstriped(offs2)] = np.tile(f64(wgs), (H // 128, 1)) * h
    x = f64(rv)[:, None] * np.abs(page[:, unstriped(offs3)])
    pq = mxq(page, 0, "e4m3")
    xq = mxq(x, 0, "e4m3")
    e = pq.T @ xq
    return e + f64(slot)[:, None]

@@ -1,0 +1,234 @@
+from contextlib import ExitStack
+
+import concourse.mybir as mybir
+from concourse.masks import make_identity
+
+K, K1, H, T, S, T2, NX = 2048, 1024, 1024, 2048, 512, 1024, 512
+FLOPS = 2 * K * H * S + 2 * H * T2 * NX
+
+F32 = mybir.dt.float32
+BF16 = mybir.dt.bfloat16
+I32 = mybir.dt.int32
+U32 = mybir.dt.uint32
+U16 = mybir.dt.uint16
+U8 = mybir.dt.uint8
+FP8X4 = mybir.dt.float8_e4m3fn_x4
+FP4X4 = mybir.dt.float4_e2m1fn_x4
+ACT = mybir.ActivationFunctionType
+ALU = mybir.AluOpType
+
+P = 128
+SLICES = H // P
+AHEAD = 2
+
+
+def tile_list_linen_wear_register_kernel(
+    tc, tab_words, tab_scales, offs, w1, w4_words, w4_scales, gain, page0, wgs, offs2, offs3, rv, slot, out
+):
+    nc = tc.nc
+    with ExitStack() as ctx:
+        keep = ctx.enter_context(tc.tile_pool(name="keep", bufs=1))
+        ring = ctx.enter_context(tc.tile_pool(name="ring", bufs=3))
+        psum = ctx.enter_context(tc.psum_pool(name="psum", bufs=1))
+
+        def bank(i, dtype=F32):
+            return psum.tile([P, 512], dtype, name="bank%d" % i, tag="bank%d" % i)
+
+        idx = keep.tile([P, S // 16], U16, name="idx")
+        idx2 = keep.tile([P, S // 16], U16, name="idx2")
+        idx3 = keep.tile([P, NX // 16], U16, name="idx3")
+
+        tab = [keep.tile([P, T], U32, name="tab%d" % a, align_bytes=64) for a in range(4)]
+        tab_sc = keep.tile([P, T], U8, name="tab_sc", align_bytes=64)
+        w4 = keep.tile([P, 2, 2 * H], U8, name="w4", align_bytes=64)
+        w4_sc = keep.tile([P, 2, H], U8, name="w4_sc", align_bytes=64)
+        v_sc3 = keep.tile([P, S], U8, name="v_sc3", align_bytes=64)
+        rows = keep.tile([P, P], F32, name="rows")
+        wgs_t = keep.tile([P, S], F32, name="wgs_t")
+        pages = [keep.tile([P, T2], F32, name="page%d" % s) for s in range(SLICES)]
+        w1_raw = [keep.tile([P, 2, 4, P], F32, name="w1_raw%d" % s, tag="w1_raw%d" % s) for s in range(SLICES)]
+
+        nc.vector.memset(tab_sc[:].bitcast(I32), 0)
+        nc.vector.memset(w4_sc[:].rearrange("p a n -> p (a n)").bitcast(I32), 0)
+        nc.vector.memset(v_sc3[:].bitcast(I32), 0)
+        nc.gpsimd.memset(rows[:], 0.0)
+        for i, vec in enumerate((gain, rv, slot)):
+            nc.gpsimd.dma_start(out=rows[8 * i : 8 * i + 8, :], in_=vec.rearrange("(s p) -> s p", p=P))
+        ident = keep.tile([P, P], F32, name="ident")
+        make_identity(nc, ident[:])
+        ident_bf = keep.tile([P, P], BF16, name="ident_bf")
+        make_identity(nc, ident_bf[:])
+
+        def load_tab(a):
+            nc.sync.dma_start(out=tab[a][:].bitcast(I32), in_=tab_words[a].rearrange("p t i -> p (t i)").bitcast(I32))
+
+        def load_w1(s):
+            for a in range(2):
+                src = w1[512 * a : 512 * (a + 1), P * s : P * (s + 1)]
+                nc.sync.dma_start(out=w1_raw[s][:, a, :, :], in_=src.rearrange("(p j) c -> p j c", j=4))
+
+        def load_page(s):
+            nc.sync.dma_start(out=pages[s][:], in_=page0[P * s : P * (s + 1), :])
+
+        load_tab(2)
+        load_tab(3)
+        nc.sync.dma_start(idx[:], offs)
+        for q in range(4):
+            for half, a0 in enumerate((2, 0)):
+                nc.sync.dma_start(
+                    out=tab_sc[32 * q + 8 * half : 32 * q + 8 * half + 8, :].bitcast(I32),
+                    in_=tab_scales[a0 : a0 + 2, 4 * q : 4 * q + 4, :].bitcast(I32),
+                )
+        nc.sync.dma_start(out=wgs_t[:], in_=wgs)
+        load_tab(0)
+        for q in range(4):
+            nc.sync.dma_start(
+                out=w4_sc[32 * q : 32 * q + 4, :, :].bitcast(I32),
+                in_=w4_scales[:, 4 * q : 4 * q + 4, :].rearrange("a r n -> r a n").bitcast(I32),
+            )
+        nc.sync.dma_start(out=w4[:].bitcast(I32), in_=w4_words.rearrange("a p n -> p a n").bitcast(I32))
+        load_w1(0)
+        load_tab(1)
+        load_w1(1)
+        load_page(0)
+        nc.sync.dma_start(idx2[:], offs2)
+        nc.sync.dma_start(idx3[:], offs3)
+        for s in range(1, SLICES):
+            if s + 1 < SLICES:
+                load_w1(s + 1)
+            load_page(s)
+
+        turned = bank(7)
+        nc.tensor.transpose(turned[:, 0:P], rows[:], ident[:])
+        vecs = keep.tile([P, 24], F32, name="vecs")
+        nc.scalar.copy(vecs[:], turned[:, 0:24])
+        gw = [keep.tile([P, S], F32, name="gw%d" % s) for s in range(SLICES)]
+        for s in range(SLICES):
+            nc.scalar.activation(gw[s][:], wgs_t[:], ACT.Copy, scale=vecs[:, s : s + 1])
+
+        v_sc = keep.tile([P, S], U8, name="v_sc", align_bytes=64)
+        nc.vector.tensor_copy(v_sc[:], tab_sc[:].indirect(idx[:]))
+        for q in range(4):
+            nc.gpsimd.dma_start(
+                out=v_sc3[32 * q : 32 * q + 4, :].bitcast(I32), in_=v_sc[32 * q + 4 : 32 * q + 8, :].bitcast(I32)
+            )
+        v = [keep.tile([P, S], U32, name="v%d" % a, align_bytes=64) for a in range(4)]
+        for a in (2, 3, 0, 1):
+            nc.vector.tensor_copy(v[a][:], tab[a][:].indirect(idx[:]))
+        v_plane = [v_sc[8:P, :], v_sc[12:P, :], v_sc[:, :], v_sc3[:, :]]
+
+        feats = {}
+
+        def features(s):
+            grouped = ring.tile([P, 2, P, 4], BF16, name="w1_grouped", align_bytes=64)
+            nc.scalar.copy(
+                grouped[:].rearrange("p a (c i) j -> p a c j i", i=4),
+                w1_raw[s][:].rearrange("p a j (c i) -> p a c j i", i=4),
+            )
+            codes = ring.tile([P, 2 * P], U32, name="w1_codes", align_bytes=64)
+            scales = ring.tile([P, 2 * P], U8, name="w1_scales", align_bytes=64)
+            nc.vector.quantize_mx(
+                out=codes[:].bitcast(FP8X4), scales=scales[:], in_=grouped[:].rearrange("p a c j -> p (a c j)")
+            )
+            f = bank(s % 2)
+            for n, a in enumerate((2, 3, 0, 1)):
+                if a >= 2:
+                    lhsT = w4[:, a - 2, 2 * P * s : 2 * P * (s + 1)].bitcast(FP4X4)
+                    lhsT_scale = w4_sc[:, a - 2, P * s : P * (s + 1)]
+                else:
+                    lhsT = codes[:, P * a : P * (a + 1)].bitcast(FP8X4)
+                    lhsT_scale = scales[:, P * a : P * (a + 1)]
+                nc.tensor.matmul_mx(
+                    out=f[:], lhsT=lhsT, lhsT_scale=lhsT_scale, rhs=v[a][:].bitcast(FP8X4), rhs_scale=v_plane[a],
+                    start=(n == 0), stop=(n == 3),
+                )
+            th = ring.tile([P, S], F32, name="th", bufs=4)
+            nc.scalar.activation(th[:], f[:], ACT.Tanh)
+            feats[s] = th
+
+        page_t = [[keep.tile([P, 4, 512], BF16, name="page_t%d%d" % (b, hf)) for hf in range(2)] for b in range(2)]
+        x_t = [keep.tile([P, 4, 512], BF16, name="x_t%d" % b) for b in range(2)]
+
+        def laid(dst, q):
+            return dst[:].rearrange("p c (u g i) -> p c g u i", u=2, i=16)[:, :, 4 * q : 4 * q + 4, :, :]
+
+        def turn_rows(s):
+            b, q = divmod(s, 4)
+            picked = ring.tile([P, NX], F32, name="picked")
+            nc.vector.tensor_copy(picked[:], pages[s][:].indirect(idx3[:]))
+            for hf in range(2):
+                pt = bank(2 + hf)
+                for c in range(4):
+                    m0 = P * (4 * hf + c)
+                    nc.tensor.transpose(pt[:, P * c : P * (c + 1)], pages[s][:, m0 : m0 + P], ident[:])
+                nc.scalar.copy(laid(page_t[b][hf], q), pt[:].rearrange("p (c g u i) -> p c g u i", c=4, u=2, i=16))
+            size = ring.tile([P, NX], F32, name="size")
+            nc.scalar.activation(size[:], picked[:], ACT.Abs)
+            xb = ring.tile([P, NX], BF16, name="xb")
+            nc.scalar.activation(xb[:], size[:], ACT.Copy, scale=vecs[:, 8 + s : 9 + s])
+            xt = bank(4, BF16)
+            for c in range(4):
+                nc.tensor.transpose(xt[:, P * c : P * (c + 1)], xb[:, P * c : P * (c + 1)], ident_bf[:])
+            nc.scalar.copy(laid(x_t[b], q), xt[:].rearrange("p (c g u i) -> p c g u i", c=4, u=2, i=16))
+
+        def turn_back(src, c0, dst, bank_no, engine):
+            words = src[:].rearrange("p c n -> p (c n)").bitcast(F32)
+            back = bank(bank_no)
+            for c in range(2):
+                for u in range(2):
+                    w0 = 256 * (c0 + c) + P * u
+                    nc.tensor.transpose(back[:, P * (2 * c + u) : P * (2 * c + u + 1)], words[:, w0 : w0 + P], ident[:])
+            o = dst.rearrange("p (c m u) -> p c m u", c=2, u=2)
+            i = back[:].rearrange("p (c u m) -> p c m u", c=2, u=2)
+            if engine == "scalar":
+                nc.scalar.copy(o, i)
+            else:
+                nc.vector.tensor_copy(o, i)
+
+        page_q, x_q = {}, {}
+
+        def quantise_pass(b):
+            other = "vector" if b == 1 else "scalar"
+            xg = keep.tile([P, 2 * NX], F32, name="xg%d" % b, align_bytes=64)
+            pg = [keep.tile([P, 512], F32, name="pg%d%d" % (b, k), align_bytes=64) for k in range(4)]
+            turn_back(page_t[b][0], 0, pg[0][:], 5, other)
+            for k in range(2):
+                turn_back(x_t[b], 2 * k, xg[:, 512 * k : 512 * (k + 1)], 6 + k, ("scalar", other)[k])
+            codes = keep.tile([P, NX], U32, name="x_codes%d" % b, align_bytes=64)
+            scales = keep.tile([P, NX], U8, name="x_scales%d" % b, align_bytes=64)
+            nc.vector.quantize_mx(out=codes[:].bitcast(FP8X4), scales=scales[:], in_=xg[:].bitcast(BF16))
+            x_q[b] = (codes, scales)
+            for k in range(4):
+                if k > 0:
+                    turn_back(page_t[b][k // 2], 2 * (k % 2), pg[k][:], 5 + k % 3, "scalar")
+                codes = keep.tile([P, 2 * P], U32, name="p_codes%d%d" % (b, k), align_bytes=64)
+                scales = keep.tile([P, 2 * P], U8, name="p_scales%d%d" % (b, k), align_bytes=64)
+                nc.vector.quantize_mx(out=codes[:].bitcast(FP8X4), scales=scales[:], in_=pg[k][:].bitcast(BF16))
+                page_q[b, k] = (codes, scales)
+
+        for s in range(AHEAD):
+            features(s)
+        for s in range(SLICES):
+            nc.vector.tensor_tensor(pages[s][:].indirect(idx2[:]), feats[s][:], gw[s][:], ALU.mult)
+            if s + AHEAD < SLICES:
+                features(s + AHEAD)
+            turn_rows(s)
+            if s % 4 == 3:
+                quantise_pass(s // 4)
+
+        for mb in range(T2 // P):
+            e = bank(mb % 5)
+            cols = slice(P * (mb % 2), P * (mb % 2 + 1))
+            for b in range(2):
+                codes, scales = page_q[b, mb // 2]
+                nc.tensor.matmul_mx(
+                    out=e[:], lhsT=codes[:, cols].bitcast(FP8X4), lhsT_scale=scales[:, cols],
+                    rhs=x_q[b][0][:].bitcast(FP8X4), rhs_scale=x_q[b][1][:], start=(b == 0), stop=(b == 1),
+                )
+            res = keep.tile([P, NX], F32, name="res%d" % mb, tag="w1_raw%d" % mb)
+            bias = vecs[:, 16 + mb : 17 + mb]
+            if mb % 2 == 0:
+                nc.scalar.activation(res[:], e[:], ACT.Identity, bias=bias)
+            else:
+                nc.vector.tensor_scalar(res[:], e[:], bias, None, ALU.add)
+            nc.sync.dma_start(out=out[P * mb : P * (mb + 1), :], in_=res[:])

@@ -19,7 +19,8 @@ ALU = mybir.AluOpType
 
 P = 128
 SLICES = H // P
-AHEAD = 2
+AHEAD = 3
+POOL_SLICES = 0
 
 
 def tile_list_linen_wear_register_kernel(
@@ -39,19 +40,19 @@ def tile_list_linen_wear_register_kernel(
         idx3 = keep.tile([P, NX // 16], U16, name="idx3")
 
         tab = [keep.tile([P, T], U32, name="tab%d" % a, align_bytes=64) for a in range(4)]
-        tab_sc = keep.tile([P, T], U8, name="tab_sc", align_bytes=64)
-        w4 = keep.tile([P, 2, 2 * H], U8, name="w4", align_bytes=64)
-        w4_sc = keep.tile([P, 2, H], U8, name="w4_sc", align_bytes=64)
-        v_sc3 = keep.tile([P, S], U8, name="v_sc3", align_bytes=64)
+        tab_sc = keep.tile([P, 2 * T], U8, name="tab_sc", align_bytes=64)
+        w4 = [keep.tile([P, 2, H], U8, name="w4_%d" % b, align_bytes=64) for b in range(2)]
+        w4_sc = [keep.tile([P, 2, H // 2], U8, name="w4_sc%d" % b, align_bytes=64) for b in range(2)]
         rows = keep.tile([P, P], F32, name="rows")
         wgs_t = keep.tile([P, S], F32, name="wgs_t")
         pages = [keep.tile([P, T2], F32, name="page%d" % s) for s in range(SLICES)]
         w1_raw = [keep.tile([P, 2, 4, P], F32, name="w1_raw%d" % s, tag="w1_raw%d" % s) for s in range(SLICES)]
 
-        nc.vector.memset(tab_sc[:].bitcast(I32), 0)
-        nc.vector.memset(w4_sc[:].rearrange("p a n -> p (a n)").bitcast(I32), 0)
-        nc.vector.memset(v_sc3[:].bitcast(I32), 0)
+        nc.gpsimd.memset(tab_sc[:, 0:T].bitcast(I32), 0)
+        nc.vector.memset(tab_sc[:, T : 2 * T].bitcast(I32), 0)
         nc.gpsimd.memset(rows[:], 0.0)
+        for b in range(2):
+            nc.vector.memset(w4_sc[b][:].rearrange("p a n -> p (a n)").bitcast(I32), 0)
         for i, vec in enumerate((gain, rv, slot)):
             nc.gpsimd.dma_start(out=rows[8 * i : 8 * i + 8, :], in_=vec.rearrange("(s p) -> s p", p=P))
         ident = keep.tile([P, P], F32, name="ident")
@@ -62,79 +63,101 @@ def tile_list_linen_wear_register_kernel(
         def load_tab(a):
             nc.sync.dma_start(out=tab[a][:].bitcast(I32), in_=tab_words[a].rearrange("p t i -> p (t i)").bitcast(I32))
 
-        def load_w1(s):
+        def load_w1(s, pieces):
+            rows_a_piece = 8 // pieces
             for a in range(2):
-                src = w1[512 * a : 512 * (a + 1), P * s : P * (s + 1)]
-                nc.sync.dma_start(out=w1_raw[s][:, a, :, :], in_=src.rearrange("(p j) c -> p j c", j=4))
+                src = w1[512 * a : 512 * (a + 1), P * s : P * (s + 1)].rearrange("(p j) c -> p j c", j=4)
+                for j in range(0, 4, rows_a_piece):
+                    nc.sync.dma_start(out=w1_raw[s][:, a, j : j + rows_a_piece, :], in_=src[:, j : j + rows_a_piece, :])
 
-        def load_page(s):
-            nc.sync.dma_start(out=pages[s][:], in_=page0[P * s : P * (s + 1), :])
+        def load_page(s, pieces):
+            width = T2 // pieces
+            for c in range(0, T2, width):
+                nc.sync.dma_start(out=pages[s][:, c : c + width], in_=page0[P * s : P * (s + 1), c : c + width])
 
-        load_tab(2)
-        load_tab(3)
-        nc.sync.dma_start(idx[:], offs)
-        for q in range(4):
-            for half, a0 in enumerate((2, 0)):
+        def load_w4(b):
+            src = w4_words[:, :, H * b : H * (b + 1)]
+            nc.sync.dma_start(out=w4[b][:].bitcast(I32), in_=src.rearrange("a p n -> p a n").bitcast(I32))
+            for q in range(4):
+                src = w4_scales[:, 4 * q : 4 * q + 4, 512 * b : 512 * (b + 1)]
                 nc.sync.dma_start(
-                    out=tab_sc[32 * q + 8 * half : 32 * q + 8 * half + 8, :].bitcast(I32),
-                    in_=tab_scales[a0 : a0 + 2, 4 * q : 4 * q + 4, :].bitcast(I32),
+                    out=w4_sc[b][32 * q : 32 * q + 4, :, :].bitcast(I32), in_=src.rearrange("a r n -> r a n").bitcast(I32)
                 )
-        nc.sync.dma_start(out=wgs_t[:], in_=wgs)
+
         load_tab(0)
         for q in range(4):
             nc.sync.dma_start(
-                out=w4_sc[32 * q : 32 * q + 4, :, :].bitcast(I32),
-                in_=w4_scales[:, 4 * q : 4 * q + 4, :].rearrange("a r n -> r a n").bitcast(I32),
+                out=tab_sc[32 * q + 4 : 32 * q + 12, 0:T].bitcast(I32),
+                in_=tab_scales[0:2, 4 * q : 4 * q + 4, :].bitcast(I32),
             )
-        nc.sync.dma_start(out=w4[:].bitcast(I32), in_=w4_words.rearrange("a p n -> p a n").bitcast(I32))
-        load_w1(0)
+        nc.sync.dma_start(idx[:], offs)
         load_tab(1)
-        load_w1(1)
-        load_page(0)
+        for q in range(4):
+            nc.sync.dma_start(
+                out=tab_sc[32 * q : 32 * q + 4, :].bitcast(I32).rearrange("r (a n) -> r a n", a=2),
+                in_=tab_scales[2:4, 4 * q : 4 * q + 4, :].rearrange("a r n -> r a n").bitcast(I32),
+            )
+        load_w1(0, 2)
+        nc.sync.dma_start(out=wgs_t[:], in_=wgs)
+        load_tab(2)
+        load_w4(0)
+        load_tab(3)
+        load_w1(1, 2)
+        load_page(0, 1)
         nc.sync.dma_start(idx2[:], offs2)
         nc.sync.dma_start(idx3[:], offs3)
-        for s in range(1, SLICES):
-            if s + 1 < SLICES:
-                load_w1(s + 1)
-            load_page(s)
+        for s in range(2, 5):
+            load_w1(s, 2)
+        load_page(1, 1)
+        load_w4(1)
+        for s in range(2, SLICES):
+            if s + 3 < SLICES:
+                load_w1(s + 3, 2 if s == 2 else 4)
+            load_page(s, (1, 4, 4, 8, 8, 8)[s - 2])
+
+        v = [keep.tile([P, S], U32, name="v%d" % a, align_bytes=64) for a in range(4)]
+        v_sc = [keep.tile([P, S], U8, name="v_sc%d" % i, align_bytes=64) for i in range(2)]
+        for a in range(4):
+            nc.vector.tensor_copy(v[a][:], tab[a][:].indirect(idx[:]))
+            if a < 2:
+                nc.vector.tensor_copy(v_sc[a][:], tab_sc[:, T * a : T * (a + 1)].indirect(idx[:]))
+        v_plane = [v_sc[0][4:P, :], v_sc[0][8:P, :], v_sc[0][:, :], v_sc[1][:, :]]
 
         turned = bank(7)
         nc.tensor.transpose(turned[:, 0:P], rows[:], ident[:])
         vecs = keep.tile([P, 24], F32, name="vecs")
         nc.scalar.copy(vecs[:], turned[:, 0:24])
-        gw = [keep.tile([P, S], F32, name="gw%d" % s) for s in range(SLICES)]
-        for s in range(SLICES):
-            nc.scalar.activation(gw[s][:], wgs_t[:], ACT.Copy, scale=vecs[:, s : s + 1])
 
-        v_sc = keep.tile([P, S], U8, name="v_sc", align_bytes=64)
-        nc.vector.tensor_copy(v_sc[:], tab_sc[:].indirect(idx[:]))
-        for q in range(4):
-            nc.gpsimd.dma_start(
-                out=v_sc3[32 * q : 32 * q + 4, :].bitcast(I32), in_=v_sc[32 * q + 4 : 32 * q + 8, :].bitcast(I32)
-            )
-        v = [keep.tile([P, S], U32, name="v%d" % a, align_bytes=64) for a in range(4)]
-        for a in (2, 3, 0, 1):
-            nc.vector.tensor_copy(v[a][:], tab[a][:].indirect(idx[:]))
-        v_plane = [v_sc[8:P, :], v_sc[12:P, :], v_sc[:, :], v_sc3[:, :]]
+        w1_q = {}
 
-        feats = {}
+        w1_bf = {}
 
-        def features(s):
-            grouped = ring.tile([P, 2, P, 4], BF16, name="w1_grouped", align_bytes=64)
+        def round_w1(s):
+            slot_name = "grouped%d" % (s % 3)
+            grouped = keep.tile([P, 2, P, 4], BF16, name="w1_grouped%d" % s, tag=slot_name, align_bytes=64)
             nc.scalar.copy(
                 grouped[:].rearrange("p a (c i) j -> p a c j i", i=4),
                 w1_raw[s][:].rearrange("p a j (c i) -> p a c j i", i=4),
             )
-            codes = ring.tile([P, 2 * P], U32, name="w1_codes", align_bytes=64)
-            scales = ring.tile([P, 2 * P], U8, name="w1_scales", align_bytes=64)
+            w1_bf[s] = grouped
+
+        def quantise_w1(s):
+            codes = keep.tile([P, 2 * P], U32, name="w1_codes%d" % s, tag="gw%d" % ((s - 2) % (SLICES + 2)), align_bytes=64)
+            scales = keep.tile([P, 2 * P], U8, name="w1_scales%d" % s, align_bytes=64)
             nc.vector.quantize_mx(
-                out=codes[:].bitcast(FP8X4), scales=scales[:], in_=grouped[:].rearrange("p a c j -> p (a c j)")
+                out=codes[:].bitcast(FP8X4), scales=scales[:], in_=w1_bf[s][:].rearrange("p a c j -> p (a c j)")
             )
+            w1_q[s] = (codes, scales)
+
+        feats = {}
+
+        def features(s):
+            codes, scales = w1_q[s]
             f = bank(s % 2)
-            for n, a in enumerate((2, 3, 0, 1)):
+            for n, a in enumerate((0, 1, 2, 3) if s == 0 else (2, 3, 0, 1)):
                 if a >= 2:
-                    lhsT = w4[:, a - 2, 2 * P * s : 2 * P * (s + 1)].bitcast(FP4X4)
-                    lhsT_scale = w4_sc[:, a - 2, P * s : P * (s + 1)]
+                    lhsT = w4[s // 4][:, a - 2, 2 * P * (s % 4) : 2 * P * (s % 4 + 1)].bitcast(FP4X4)
+                    lhsT_scale = w4_sc[s // 4][:, a - 2, P * (s % 4) : P * (s % 4 + 1)]
                 else:
                     lhsT = codes[:, P * a : P * (a + 1)].bitcast(FP8X4)
                     lhsT_scale = scales[:, P * a : P * (a + 1)]
@@ -142,34 +165,74 @@ def tile_list_linen_wear_register_kernel(
                     out=f[:], lhsT=lhsT, lhsT_scale=lhsT_scale, rhs=v[a][:].bitcast(FP8X4), rhs_scale=v_plane[a],
                     start=(n == 0), stop=(n == 3),
                 )
-            th = ring.tile([P, S], F32, name="th", bufs=4)
+            if s == 0:
+                th = keep.tile([P, S], F32, name="th0", tag="w1_raw1")
+            else:
+                th = keep.tile([P, S], F32, name="th%d" % s, tag="th%d" % (s % 3), align_bytes=64)
             nc.scalar.activation(th[:], f[:], ACT.Tanh)
             feats[s] = th
 
-        page_t = [[keep.tile([P, 4, 512], BF16, name="page_t%d%d" % (b, hf)) for hf in range(2)] for b in range(2)]
+        gw = [keep.tile([P, S], F32, name="gw%d" % s, tag="gw%d" % s, align_bytes=64) for s in range(SLICES)]
+
+        def weigh(s):
+            nc.scalar.activation(gw[s][:], wgs_t[:], ACT.Copy, scale=vecs[:, s : s + 1])
+
+        for s in range(2):
+            round_w1(s)
+            quantise_w1(s)
+        for s in range(2):
+            features(s)
+            weigh(s)
+        for s in range(2, 5):
+            round_w1(s)
+        for s in range(2, SLICES):
+            weigh(s)
+
+        page_t = [
+            [keep.tile([P, 4, 512], BF16, name="page_t%d%d" % (b, hf), tag=("w1_raw%d" % (2 + hf) if b == 0 else "page_t1%d" % hf)) for hf in range(2)]
+            for b in range(2)
+        ]
         x_t = [keep.tile([P, 4, 512], BF16, name="x_t%d" % b) for b in range(2)]
 
         def laid(dst, q):
             return dst[:].rearrange("p c (u g i) -> p c g u i", u=2, i=16)[:, :, 4 * q : 4 * q + 4, :, :]
 
-        def turn_rows(s):
+        def turn_page(s, hf, bank_no):
             b, q = divmod(s, 4)
-            picked = ring.tile([P, NX], F32, name="picked")
-            nc.vector.tensor_copy(picked[:], pages[s][:].indirect(idx3[:]))
-            for hf in range(2):
-                pt = bank(2 + hf)
-                for c in range(4):
-                    m0 = P * (4 * hf + c)
-                    nc.tensor.transpose(pt[:, P * c : P * (c + 1)], pages[s][:, m0 : m0 + P], ident[:])
-                nc.scalar.copy(laid(page_t[b][hf], q), pt[:].rearrange("p (c g u i) -> p c g u i", c=4, u=2, i=16))
-            size = ring.tile([P, NX], F32, name="size")
-            nc.scalar.activation(size[:], picked[:], ACT.Abs)
-            xb = ring.tile([P, NX], BF16, name="xb")
-            nc.scalar.activation(xb[:], size[:], ACT.Copy, scale=vecs[:, 8 + s : 9 + s])
-            xt = bank(4, BF16)
+            pt = bank(bank_no)
             for c in range(4):
-                nc.tensor.transpose(xt[:, P * c : P * (c + 1)], xb[:, P * c : P * (c + 1)], ident_bf[:])
-            nc.scalar.copy(laid(x_t[b], q), xt[:].rearrange("p (c g u i) -> p c g u i", c=4, u=2, i=16))
+                m0 = P * (4 * hf + c)
+                nc.tensor.transpose(pt[:, P * c : P * (c + 1)], pages[s][:, m0 : m0 + P], ident[:])
+            nc.scalar.copy(laid(page_t[b][hf], q), pt[:].rearrange("p (c g u i) -> p c g u i", c=4, u=2, i=16))
+
+        def turn_x_part(s, src, c0, count, bank_no):
+            b, q = divmod(s, 4)
+            xt = bank(bank_no, BF16)
+            for c in range(count):
+                nc.tensor.transpose(xt[:, P * c : P * (c + 1)], src[:, P * c : P * (c + 1)], ident_bf[:])
+            nc.scalar.copy(
+                laid(x_t[b], q)[:, c0 : c0 + count],
+                xt[:, 0 : P * count].rearrange("p (c g u i) -> p c g u i", c=count, u=2, i=16),
+            )
+
+        def turn_x(s):
+            picked = keep.tile([P, NX], F32, name="picked%d" % s, tag="picked%d" % (s % 2), align_bytes=64)
+            nc.vector.tensor_copy(picked[:], pages[s][:].indirect(idx3[:]))
+            if s + 2 < SLICES:
+                quantise_w1(s + 2)
+                features(s + 2)
+            if 4 < s + 4 < SLICES:
+                round_w1(s + 4)
+            turn_page(s, 0, 2)
+            turn_page(s, 1, 3)
+            size = keep.tile([P, NX], F32, name="size%d" % s, tag="w1_raw4" if s == 0 else "size%d" % (s % 2))
+            nc.scalar.activation(size[:], picked[:], ACT.Abs)
+            xb = keep.tile([P, NX], BF16, name="xb%d" % s, tag="xb%d" % (s % 2))
+            if s < POOL_SLICES:
+                nc.gpsimd.tensor_scalar(xb[:], size[:], vecs[:, 8 + s : 9 + s], 0.0, ALU.mult, ALU.add)
+            else:
+                nc.scalar.activation(xb[:], size[:], ACT.Copy, scale=vecs[:, 8 + s : 9 + s])
+            turn_x_part(s, xb[:], 0, 4, 4)
 
         def turn_back(src, c0, dst, bank_no, engine):
             words = src[:].rearrange("p c n -> p (c n)").bitcast(F32)
@@ -187,47 +250,89 @@ def tile_list_linen_wear_register_kernel(
 
         page_q, x_q = {}, {}
 
-        def quantise_pass(b):
-            other = "vector" if b == 1 else "scalar"
-            xg = keep.tile([P, 2 * NX], F32, name="xg%d" % b, align_bytes=64)
-            pg = [keep.tile([P, 512], F32, name="pg%d%d" % (b, k), align_bytes=64) for k in range(4)]
-            turn_back(page_t[b][0], 0, pg[0][:], 5, other)
-            for k in range(2):
-                turn_back(x_t[b], 2 * k, xg[:, 512 * k : 512 * (k + 1)], 6 + k, ("scalar", other)[k])
-            codes = keep.tile([P, NX], U32, name="x_codes%d" % b, align_bytes=64)
-            scales = keep.tile([P, NX], U8, name="x_scales%d" % b, align_bytes=64)
-            nc.vector.quantize_mx(out=codes[:].bitcast(FP8X4), scales=scales[:], in_=xg[:].bitcast(BF16))
-            x_q[b] = (codes, scales)
-            for k in range(4):
-                if k > 0:
-                    turn_back(page_t[b][k // 2], 2 * (k % 2), pg[k][:], 5 + k % 3, "scalar")
-                codes = keep.tile([P, 2 * P], U32, name="p_codes%d%d" % (b, k), align_bytes=64)
-                scales = keep.tile([P, 2 * P], U8, name="p_scales%d%d" % (b, k), align_bytes=64)
-                nc.vector.quantize_mx(out=codes[:].bitcast(FP8X4), scales=scales[:], in_=pg[k][:].bitcast(BF16))
-                page_q[b, k] = (codes, scales)
+        def quantise_page(k, bank_no, engine):
+            pg = keep.tile([P, 512], F32, name="pg1%d" % k, align_bytes=64)
+            turn_back(page_t[1][k // 2], 2 * (k % 2), pg[:], bank_no, engine)
+            codes = keep.tile([P, 2 * P], U32, name="p_codes1%d" % k, align_bytes=64)
+            scales = keep.tile([P, 2 * P], U8, name="p_scales1%d" % k, align_bytes=64)
+            nc.vector.quantize_mx(out=codes[:].bitcast(FP8X4), scales=scales[:], in_=pg[:].bitcast(BF16))
+            page_q[1, k] = (codes[:], scales[:])
 
-        for s in range(AHEAD):
-            features(s)
+        def score_pass(e, mb, b):
+            cols = slice(P * (mb % 2), P * (mb % 2 + 1))
+            codes, scales = page_q[b, mb // 2]
+            nc.tensor.matmul_mx(
+                out=e[:], lhsT=codes[:, cols].bitcast(FP8X4), lhsT_scale=scales[:, cols],
+                rhs=x_q[b][0][:].bitcast(FP8X4), rhs_scale=x_q[b][1][:], start=(b == 0), stop=(b == 1),
+            )
+
+        early = {}
+        last = SLICES - 1
         for s in range(SLICES):
             nc.vector.tensor_tensor(pages[s][:].indirect(idx2[:]), feats[s][:], gw[s][:], ALU.mult)
-            if s + AHEAD < SLICES:
-                features(s + AHEAD)
-            turn_rows(s)
-            if s % 4 == 3:
-                quantise_pass(s // 4)
+            if s < last:
+                turn_x(s)
+            if s == 3:
+                xg0 = keep.tile([P, 2 * NX], F32, name="xg0", align_bytes=64)
+                pg0 = keep.tile([P, 2 * T2], F32, name="pg0", align_bytes=64)
+                for k in range(2):
+                    turn_back(x_t[0], 2 * k, xg0[:, 512 * k : 512 * (k + 1)], 5 + k, "scalar")
+            if s in (4, 5):
+                for k in (2 * s - 8, 2 * s - 7):
+                    turn_back(page_t[0][k // 2], 2 * (k % 2), pg0[:, 512 * k : 512 * (k + 1)], 5 + (k + 2) % 3, "scalar")
+            if s == 5:
+                codes = keep.tile([P, NX], U32, name="x_codes0", tag="th2", align_bytes=64)
+                scales = keep.tile([P, NX], U8, name="x_scales0", align_bytes=64)
+                nc.vector.quantize_mx(out=codes[:].bitcast(FP8X4), scales=scales[:], in_=xg0[:].bitcast(BF16))
+                x_q[0] = (codes, scales)
+            if s == 6:
+                codes = keep.tile([P, T2], U32, name="p_codes0", tag="gw6", align_bytes=64)
+                scales = keep.tile([P, T2], U8, name="p_scales0", align_bytes=64)
+                nc.vector.quantize_mx(out=codes[:].bitcast(FP8X4), scales=scales[:], in_=pg0[:].bitcast(BF16))
+                for k in range(4):
+                    page_q[0, k] = (codes[:, 256 * k : 256 * (k + 1)], scales[:, 256 * k : 256 * (k + 1)])
+        for mb, bank_no in enumerate((7, 0, 1)):
+            early[mb] = bank(bank_no)
+            score_pass(early[mb], mb, 0)
+
+        half = NX // 2
+        picked = [keep.tile([P, half], F32, name="picked7%d" % hf, tag="picked7%d" % hf) for hf in range(2)]
+        size = [keep.tile([P, half], F32, name="size7%d" % hf) for hf in range(2)]
+        xb = [keep.tile([P, half], BF16, name="xb7%d" % hf) for hf in range(2)]
+        for hf in range(2):
+            nc.vector.tensor_copy(picked[hf][:], pages[last][:].indirect(idx3[:, 16 * hf : 16 * (hf + 1)]))
+        turn_page(last, 0, 2)
+        for hf in range(2):
+            nc.scalar.activation(size[hf][:], picked[hf][:], ACT.Abs)
+            nc.vector.tensor_scalar(xb[hf][:], size[hf][:], vecs[:, 8 + last : 9 + last], None, ALU.mult)
+        xg = keep.tile([P, 2 * NX], F32, name="xg1", align_bytes=64)
+        codes = keep.tile([P, NX], U32, name="x_codes1", align_bytes=64)
+        scales = keep.tile([P, NX], U8, name="x_scales1", align_bytes=64)
+        x_q[1] = (codes, scales)
+        for hf in range(2):
+            turn_x_part(last, xb[hf][:], 2 * hf, 2, 4 + hf)
+        for hf in range(2):
+            turn_back(x_t[1], 2 * hf, xg[:, 512 * hf : 512 * (hf + 1)], (6, 4)[hf], ("scalar", "vector")[hf])
+            cols = slice(half * hf, half * (hf + 1))
+            nc.vector.quantize_mx(
+                out=codes[:, cols].bitcast(FP8X4), scales=scales[:, cols], in_=xg[:, 512 * hf : 512 * (hf + 1)].bitcast(BF16)
+            )
+        quantise_page(0, 2, "vector")
+        turn_page(last, 1, 3)
+        quantise_page(1, 5, "scalar")
+        quantise_page(2, 3, "vector")
+        quantise_page(3, 6, "scalar")
 
         for mb in range(T2 // P):
-            e = bank(mb % 5)
-            cols = slice(P * (mb % 2), P * (mb % 2 + 1))
-            for b in range(2):
-                codes, scales = page_q[b, mb // 2]
-                nc.tensor.matmul_mx(
-                    out=e[:], lhsT=codes[:, cols].bitcast(FP8X4), lhsT_scale=scales[:, cols],
-                    rhs=x_q[b][0][:].bitcast(FP8X4), rhs_scale=x_q[b][1][:], start=(b == 0), stop=(b == 1),
-                )
-            res = keep.tile([P, NX], F32, name="res%d" % mb, tag="w1_raw%d" % mb)
+            if mb in early:
+                e = early[mb]
+            else:
+                e = bank((2, 4, 5, 3, 6)[mb - 3])
+                score_pass(e, mb, 0)
+            score_pass(e, mb, 1)
+            res = keep.tile([P, NX], F32, name="res%d" % mb, tag="gw%d" % mb if mb < 6 else "res%d" % mb, align_bytes=64)
             bias = vecs[:, 16 + mb : 17 + mb]
-            if mb % 2 == 0:
+            if mb % 3 != 1:
                 nc.scalar.activation(res[:], e[:], ACT.Identity, bias=bias)
             else:
                 nc.vector.tensor_scalar(res[:], e[:], bias, None, ALU.add)

@@ -20,7 +20,7 @@ ALU = mybir.AluOpType
 P = 128
 SLICES = H // P
 AHEAD = 3
-POOL_SLICES = 0
+PIECES = (1, 1, 1, 4, 2, 2, 2, 8)
 
 
 def tile_list_linen_wear_register_kernel(
@@ -29,7 +29,6 @@ def tile_list_linen_wear_register_kernel(
     nc = tc.nc
     with ExitStack() as ctx:
         keep = ctx.enter_context(tc.tile_pool(name="keep", bufs=1))
-        ring = ctx.enter_context(tc.tile_pool(name="ring", bufs=3))
         psum = ctx.enter_context(tc.psum_pool(name="psum", bufs=1))
 
         def bank(i, dtype=F32):
@@ -40,110 +39,152 @@ def tile_list_linen_wear_register_kernel(
         idx3 = keep.tile([P, NX // 16], U16, name="idx3")
 
         tab = [keep.tile([P, T], U32, name="tab%d" % a, align_bytes=64) for a in range(4)]
-        tab_sc = keep.tile([P, 2 * T], U8, name="tab_sc", align_bytes=64)
+        tab_sc = keep.tile([P, T], U8, name="tab_sc", align_bytes=64)
+        v_sc23 = keep.tile([P, 2, S], U8, name="v_sc23", align_bytes=64)
         w4 = [keep.tile([P, 2, H], U8, name="w4_%d" % b, align_bytes=64) for b in range(2)]
         w4_sc = [keep.tile([P, 2, H // 2], U8, name="w4_sc%d" % b, align_bytes=64) for b in range(2)]
-        rows = keep.tile([P, P], F32, name="rows")
+        rows = [keep.tile([P, P], F32, name="rows%d" % i) for i in range(2)]
         wgs_t = keep.tile([P, S], F32, name="wgs_t")
         pages = [keep.tile([P, T2], F32, name="page%d" % s) for s in range(SLICES)]
-        w1_raw = [keep.tile([P, 2, 4, P], F32, name="w1_raw%d" % s, tag="w1_raw%d" % s) for s in range(SLICES)]
+        w1_raw = [keep.tile([P, 2, 4, 2 * P], F32, name="w1_raw%d" % d, tag="w1_raw%d" % d) for d in range(2)]
+        w1_raw.append(keep.tile([P, 2, 4, 4 * P], F32, name="w1_raw2"))
+        wgs_dealt = [keep.tile([P, S], F32, name="wgs_dealt%d" % t) for t in range(4)]
 
-        nc.gpsimd.memset(tab_sc[:, 0:T].bitcast(I32), 0)
-        nc.vector.memset(tab_sc[:, T : 2 * T].bitcast(I32), 0)
-        nc.gpsimd.memset(rows[:], 0.0)
+        nc.gpsimd.memset(tab_sc[:, 0 : T // 2].bitcast(I32), 0)
+        nc.vector.memset(tab_sc[:, T // 2 : T].bitcast(I32), 0)
+        nc.vector.memset(v_sc23[:].rearrange("p a n -> p (a n)").bitcast(I32), 0)
+        for i in range(2):
+            nc.gpsimd.memset(rows[i][:], 0.0)
         for b in range(2):
             nc.vector.memset(w4_sc[b][:].rearrange("p a n -> p (a n)").bitcast(I32), 0)
-        for i, vec in enumerate((gain, rv, slot)):
-            nc.gpsimd.dma_start(out=rows[8 * i : 8 * i + 8, :], in_=vec.rearrange("(s p) -> s p", p=P))
+        nc.gpsimd.dma_start(out=rows[0][0:4, :], in_=gain[0:512].rearrange("(s p) -> s p", p=P))
         ident = keep.tile([P, P], F32, name="ident")
         make_identity(nc, ident[:])
-        ident_bf = keep.tile([P, P], BF16, name="ident_bf")
-        make_identity(nc, ident_bf[:])
 
         def load_tab(a):
             nc.sync.dma_start(out=tab[a][:].bitcast(I32), in_=tab_words[a].rearrange("p t i -> p (t i)").bitcast(I32))
 
-        def load_w1(s, pieces):
+        def load_w1(d, c0, c1, pieces):
             rows_a_piece = 8 // pieces
             for a in range(2):
-                src = w1[512 * a : 512 * (a + 1), P * s : P * (s + 1)].rearrange("(p j) c -> p j c", j=4)
+                src = w1[512 * a : 512 * (a + 1), c0:c1].rearrange("(p j) c -> p j c", j=4)
                 for j in range(0, 4, rows_a_piece):
-                    nc.sync.dma_start(out=w1_raw[s][:, a, j : j + rows_a_piece, :], in_=src[:, j : j + rows_a_piece, :])
+                    nc.sync.dma_start(out=w1_raw[d][:, a, j : j + rows_a_piece, :], in_=src[:, j : j + rows_a_piece, :])
 
         def load_page(s, pieces):
             width = T2 // pieces
             for c in range(0, T2, width):
-                nc.sync.dma_start(out=pages[s][:, c : c + width], in_=page0[P * s : P * (s + 1), c : c + width])
+                if s < 4:
+                    src = page0[P * s : P * (s + 1), c : c + width]
+                else:
+                    src = page0[512:H, c : c + width].rearrange("(g t i) m -> t g i m", t=4, i=8)[s - 4]
+                nc.sync.dma_start(out=pages[s][:, c : c + width], in_=src)
+
+        def load_wgs_dealt(t):
+            for q in range(4):
+                src = wgs.rearrange("(g t i) j -> t g i j", t=4, i=8)[t]
+                nc.sync.dma_start(out=wgs_dealt[t][32 * q : 32 * (q + 1), :], in_=src)
 
         def load_w4(b):
             src = w4_words[:, :, H * b : H * (b + 1)]
             nc.sync.dma_start(out=w4[b][:].bitcast(I32), in_=src.rearrange("a p n -> p a n").bitcast(I32))
+
+        def load_w4_scales(b, queue):
             for q in range(4):
                 src = w4_scales[:, 4 * q : 4 * q + 4, 512 * b : 512 * (b + 1)]
-                nc.sync.dma_start(
+                queue.dma_start(
                     out=w4_sc[b][32 * q : 32 * q + 4, :, :].bitcast(I32), in_=src.rearrange("a r n -> r a n").bitcast(I32)
                 )
 
+        ident_bf = keep.tile([P, P], BF16, name="ident_bf")
+        make_identity(nc, ident_bf[:])
+
+        v_sc = keep.tile([P, S], U8, name="v_sc", align_bytes=64)
+
+        def move_plane(a):
+            for q in range(4):
+                nc.sync.dma_start(
+                    out=v_sc23[32 * q : 32 * q + 4, a - 2, :].bitcast(I32),
+                    in_=v_sc[32 * q + 4 * a : 32 * q + 4 * a + 4, :].bitcast(I32),
+                )
+
         load_tab(0)
-        for q in range(4):
-            nc.sync.dma_start(
-                out=tab_sc[32 * q + 4 : 32 * q + 12, 0:T].bitcast(I32),
-                in_=tab_scales[0:2, 4 * q : 4 * q + 4, :].bitcast(I32),
-            )
         nc.sync.dma_start(idx[:], offs)
-        load_tab(1)
         for q in range(4):
             nc.sync.dma_start(
-                out=tab_sc[32 * q : 32 * q + 4, :].bitcast(I32).rearrange("r (a n) -> r a n", a=2),
-                in_=tab_scales[2:4, 4 * q : 4 * q + 4, :].rearrange("a r n -> r a n").bitcast(I32),
+                out=tab_sc[32 * q : 32 * q + 16, :].bitcast(I32), in_=tab_scales[:, 4 * q : 4 * q + 4, :].bitcast(I32)
             )
-        load_w1(0, 2)
-        nc.sync.dma_start(out=wgs_t[:], in_=wgs)
+        nc.vector.tensor_copy(v_sc[:], tab_sc[:].indirect(idx[:]))
         load_tab(2)
-        load_w4(0)
+        load_w1(0, 0, 256, 2)
+        move_plane(2)
         load_tab(3)
-        load_w1(1, 2)
+        load_w4(0)
+        load_w4_scales(0, nc.sync)
+        load_tab(1)
+        nc.sync.dma_start(out=wgs_t[:], in_=wgs)
+        move_plane(3)
         load_page(0, 1)
         nc.sync.dma_start(idx2[:], offs2)
         nc.sync.dma_start(idx3[:], offs3)
-        for s in range(2, 5):
-            load_w1(s, 2)
-        load_page(1, 1)
+        load_w1(1, 256, 512, 2)
+        for r0, vec in ((4, gain), (12, rv)):
+            nc.sync.dma_start(
+                out=rows[1][r0 : r0 + 4, :].rearrange("t (g i) -> t g i", i=8),
+                in_=vec[512:H].rearrange("(g t i) -> t g i", t=4, i=8),
+            )
+        nc.sync.dma_start(out=rows[1][8:12, :], in_=rv[0:512].rearrange("(s p) -> s p", p=P))
+        nc.sync.dma_start(out=rows[1][16:24, :], in_=slot.rearrange("(s p) -> s p", p=P))
+        load_page(1, PIECES[1])
+        load_w1(2, 512, H, 4)
         load_w4(1)
-        for s in range(2, SLICES):
-            if s + 3 < SLICES:
-                load_w1(s + 3, 2 if s == 2 else 4)
-            load_page(s, (1, 4, 4, 8, 8, 8)[s - 2])
+        load_w4_scales(1, nc.sync)
+        load_page(2, PIECES[2])
+        load_wgs_dealt(0)
+        load_page(3, PIECES[3])
+        for s in range(4, SLICES):
+            if s < SLICES - 1:
+                load_wgs_dealt(s - 3)
+            load_page(s, PIECES[s])
 
         v = [keep.tile([P, S], U32, name="v%d" % a, align_bytes=64) for a in range(4)]
-        v_sc = [keep.tile([P, S], U8, name="v_sc%d" % i, align_bytes=64) for i in range(2)]
-        for a in range(4):
+        for a in (0, 2, 3, 1):
             nc.vector.tensor_copy(v[a][:], tab[a][:].indirect(idx[:]))
-            if a < 2:
-                nc.vector.tensor_copy(v_sc[a][:], tab_sc[:, T * a : T * (a + 1)].indirect(idx[:]))
-        v_plane = [v_sc[0][4:P, :], v_sc[0][8:P, :], v_sc[0][:, :], v_sc[1][:, :]]
+        v_plane = [v_sc[:, :], v_sc[4:P, :], v_sc23[:, 0, :], v_sc23[:, 1, :]]
 
-        turned = bank(7)
-        nc.tensor.transpose(turned[:, 0:P], rows[:], ident[:])
+        first_gains = keep.tile([P, 4], F32, name="first_gains")
         vecs = keep.tile([P, 24], F32, name="vecs")
-        nc.scalar.copy(vecs[:], turned[:, 0:24])
+        for i, dst in enumerate((first_gains, vecs)):
+            turned = bank(7 - i)
+            nc.tensor.transpose(turned[:, 0:P], rows[i][:], ident[:])
+            nc.scalar.copy(dst[:], turned[:, 0 : (4, 24)[i]])
+        signs = keep.tile([P, SLICES], F32, name="signs")
+        halves = keep.tile([P, SLICES], F32, name="halves")
+        nc.gpsimd.tensor_scalar(halves[:], vecs[:, 8:16], 0.0, 0.5, ALU.is_ge, ALU.subtract)
+        nc.gpsimd.tensor_scalar(signs[:], halves[:], 2.0, 0.0, ALU.mult, ALU.add)
 
         w1_q = {}
 
         w1_bf = {}
 
         def round_w1(s):
-            slot_name = "grouped%d" % (s % 3)
+            slot_name = "grouped%d" % (s % 2)
             grouped = keep.tile([P, 2, P, 4], BF16, name="w1_grouped%d" % s, tag=slot_name, align_bytes=64)
-            nc.scalar.copy(
-                grouped[:].rearrange("p a (c i) j -> p a c j i", i=4),
-                w1_raw[s][:].rearrange("p a j (c i) -> p a c j i", i=4),
-            )
+            if s < 4:
+                nc.scalar.copy(
+                    grouped[:].rearrange("p a (c i) j -> p a c j i", i=4),
+                    w1_raw[s // 2][:, :, :, P * (s % 2) : P * (s % 2 + 1)].rearrange("p a j (c i) -> p a c j i", i=4),
+                )
+            else:
+                nc.scalar.copy(
+                    grouped[:].rearrange("p a (g i) j -> p a g j i", i=8),
+                    w1_raw[2][:].rearrange("p a j (g t i) -> p t a g j i", t=4, i=8)[:, s - 4],
+                )
             w1_bf[s] = grouped
 
         def quantise_w1(s):
-            codes = keep.tile([P, 2 * P], U32, name="w1_codes%d" % s, tag="gw%d" % ((s - 2) % (SLICES + 2)), align_bytes=64)
-            scales = keep.tile([P, 2 * P], U8, name="w1_scales%d" % s, align_bytes=64)
+            codes = keep.tile([P, 2 * P], U32, name="w1_codes%d" % s, tag="gw%d" % (s - 2 if s > 1 else 1 + 2 * s), align_bytes=64)
+            scales = keep.tile([P, 2 * P], U8, name="w1_scales%d" % s, tag="gw2" if s == 0 else "w1_scales%d" % s, align_bytes=64)
             nc.vector.quantize_mx(
                 out=codes[:].bitcast(FP8X4), scales=scales[:], in_=w1_bf[s][:].rearrange("p a c j -> p (a c j)")
             )
@@ -151,10 +192,20 @@ def tile_list_linen_wear_register_kernel(
 
         feats = {}
 
+        def deal_w4():
+            words = keep.tile([P, 2, H], U8, name="w4_dealt", align_bytes=64)
+            scales = keep.tile([P, 2, H // 2], U8, name="w4_sc_dealt", align_bytes=64)
+            for dst, src, w in ((words, w4[1], 4), (scales, w4_sc[1], 2)):
+                nc.vector.tensor_copy(
+                    dst[:].bitcast(I32).rearrange("p a (t g w) -> p a t g w", t=4, w=w),
+                    src[:].bitcast(I32).rearrange("p a (g t w) -> p a t g w", t=4, w=w),
+                )
+            w4[1], w4_sc[1] = words, scales
+
         def features(s):
             codes, scales = w1_q[s]
             f = bank(s % 2)
-            for n, a in enumerate((0, 1, 2, 3) if s == 0 else (2, 3, 0, 1)):
+            for n, a in enumerate((0, 2, 3, 1) if s == 0 else (2, 3, 0, 1)):
                 if a >= 2:
                     lhsT = w4[s // 4][:, a - 2, 2 * P * (s % 4) : 2 * P * (s % 4 + 1)].bitcast(FP4X4)
                     lhsT_scale = w4_sc[s // 4][:, a - 2, P * (s % 4) : P * (s % 4 + 1)]
@@ -165,17 +216,16 @@ def tile_list_linen_wear_register_kernel(
                     out=f[:], lhsT=lhsT, lhsT_scale=lhsT_scale, rhs=v[a][:].bitcast(FP8X4), rhs_scale=v_plane[a],
                     start=(n == 0), stop=(n == 3),
                 )
-            if s == 0:
-                th = keep.tile([P, S], F32, name="th0", tag="w1_raw1")
-            else:
-                th = keep.tile([P, S], F32, name="th%d" % s, tag="th%d" % (s % 3), align_bytes=64)
+            th = keep.tile([P, S], F32, name="th%d" % s, tag="th%d" % (s % 4), align_bytes=64)
             nc.scalar.activation(th[:], f[:], ACT.Tanh)
             feats[s] = th
 
-        gw = [keep.tile([P, S], F32, name="gw%d" % s, tag="gw%d" % s, align_bytes=64) for s in range(SLICES)]
+        gw = {}
 
         def weigh(s):
-            nc.scalar.activation(gw[s][:], wgs_t[:], ACT.Copy, scale=vecs[:, s : s + 1])
+            src, gains = (wgs_t, first_gains) if s < 4 else (wgs_dealt[s - 4], vecs)
+            gw[s] = keep.tile([P, S], F32, name="gw%d" % s, tag="gw%d" % s, align_bytes=64)
+            nc.scalar.activation(gw[s][:], src[:], ACT.Copy, scale=gains[:, s : s + 1])
 
         for s in range(2):
             round_w1(s)
@@ -183,157 +233,186 @@ def tile_list_linen_wear_register_kernel(
         for s in range(2):
             features(s)
             weigh(s)
-        for s in range(2, 5):
+        for s in range(2, 4):
             round_w1(s)
-        for s in range(2, SLICES):
+        for s in range(2, 4):
             weigh(s)
 
-        page_t = [
-            [keep.tile([P, 4, 512], BF16, name="page_t%d%d" % (b, hf), tag=("w1_raw%d" % (2 + hf) if b == 0 else "page_t1%d" % hf)) for hf in range(2)]
-            for b in range(2)
-        ]
-        x_t = [keep.tile([P, 4, 512], BF16, name="x_t%d" % b) for b in range(2)]
+        page_t = keep.tile([P, 8, 512], BF16, name="page_t0", tag="w1_raw1")
+        x_t = keep.tile([P, 4, 512], BF16, name="x_t0")
 
         def laid(dst, q):
-            return dst[:].rearrange("p c (u g i) -> p c g u i", u=2, i=16)[:, :, 4 * q : 4 * q + 4, :, :]
+            return dst.rearrange("p c (u g i) -> p c g u i", u=2, i=16)[:, :, 4 * q : 4 * q + 4, :, :]
 
-        def turn_page(s, hf, bank_no):
-            b, q = divmod(s, 4)
-            pt = bank(bank_no)
+        def turn_rows(src, dst, q, bank_no, dtype, identity):
+            turned_rows = bank(bank_no, dtype)
             for c in range(4):
-                m0 = P * (4 * hf + c)
-                nc.tensor.transpose(pt[:, P * c : P * (c + 1)], pages[s][:, m0 : m0 + P], ident[:])
-            nc.scalar.copy(laid(page_t[b][hf], q), pt[:].rearrange("p (c g u i) -> p c g u i", c=4, u=2, i=16))
+                nc.tensor.transpose(turned_rows[:, P * c : P * (c + 1)], src[:, P * c : P * (c + 1)], identity[:])
+            nc.scalar.copy(laid(dst, q), turned_rows[:].rearrange("p (c g u i) -> p c g u i", c=4, u=2, i=16))
 
-        def turn_x_part(s, src, c0, count, bank_no):
-            b, q = divmod(s, 4)
-            xt = bank(bank_no, BF16)
-            for c in range(count):
-                nc.tensor.transpose(xt[:, P * c : P * (c + 1)], src[:, P * c : P * (c + 1)], ident_bf[:])
-            nc.scalar.copy(
-                laid(x_t[b], q)[:, c0 : c0 + count],
-                xt[:, 0 : P * count].rearrange("p (c g u i) -> p c g u i", c=count, u=2, i=16),
-            )
-
-        def turn_x(s):
-            picked = keep.tile([P, NX], F32, name="picked%d" % s, tag="picked%d" % (s % 2), align_bytes=64)
-            nc.vector.tensor_copy(picked[:], pages[s][:].indirect(idx3[:]))
-            if s + 2 < SLICES:
-                quantise_w1(s + 2)
-                features(s + 2)
-            if 4 < s + 4 < SLICES:
-                round_w1(s + 4)
-            turn_page(s, 0, 2)
-            turn_page(s, 1, 3)
-            size = keep.tile([P, NX], F32, name="size%d" % s, tag="w1_raw4" if s == 0 else "size%d" % (s % 2))
-            nc.scalar.activation(size[:], picked[:], ACT.Abs)
-            xb = keep.tile([P, NX], BF16, name="xb%d" % s, tag="xb%d" % (s % 2))
-            if s < POOL_SLICES:
-                nc.gpsimd.tensor_scalar(xb[:], size[:], vecs[:, 8 + s : 9 + s], 0.0, ALU.mult, ALU.add)
-            else:
-                nc.scalar.activation(xb[:], size[:], ACT.Copy, scale=vecs[:, 8 + s : 9 + s])
-            turn_x_part(s, xb[:], 0, 4, 4)
-
-        def turn_back(src, c0, dst, bank_no, engine):
+        def turn_back(src, c0, dst, bank_no):
             words = src[:].rearrange("p c n -> p (c n)").bitcast(F32)
             back = bank(bank_no)
             for c in range(2):
                 for u in range(2):
                     w0 = 256 * (c0 + c) + P * u
                     nc.tensor.transpose(back[:, P * (2 * c + u) : P * (2 * c + u + 1)], words[:, w0 : w0 + P], ident[:])
-            o = dst.rearrange("p (c m u) -> p c m u", c=2, u=2)
-            i = back[:].rearrange("p (c u m) -> p c m u", c=2, u=2)
-            if engine == "scalar":
-                nc.scalar.copy(o, i)
+            nc.scalar.copy(dst.rearrange("p (c m u) -> p c m u", c=2, u=2), back[:].rearrange("p (c u m) -> p c m u", c=2, u=2))
+
+        page_planes = [keep.tile([P, 4, T2 // 2], BF16, name="page_planes%d" % hf) for hf in range(2)]
+        x_planes = [keep.tile([P, 4, NX // 2], BF16, name="x_planes%d" % hf) for hf in range(2)]
+        sizes = {}
+        last = SLICES - 1
+        half = NX // 2
+
+        def sign_x(s):
+            xb = keep.tile([P, NX], BF16, name="xb%d" % s, tag="th%d" % ((s + 1) % 4), align_bytes=64)
+            nc.vector.tensor_scalar(xb[:], sizes[s][:], signs[:, s : s + 1], None, ALU.mult)
+            turn_rows(xb[:], x_t[:], s, 4, BF16, ident_bf)
+
+        picks = {}
+
+        def round_page(s, hf):
+            nc.scalar.activation(
+                page_planes[hf][:, s - 4, :], pages[s][:, 512 * hf : 512 * (hf + 1)], ACT.Copy, scale=signs[:, s : s + 1]
+            )
+
+        def size_x(s, hf):
+            nc.scalar.activation(
+                x_planes[hf][:, s - 4, :], picks[s][:, half * hf : half * (hf + 1)], ACT.Abs, scale=vecs[:, 8 + s : 9 + s]
+            )
+
+        def follow(s):
+            picked = keep.tile([P, NX], F32, name="picked%d" % s, tag="picked%d" % (s % 2), align_bytes=64)
+            picks[s] = picked
+            if s < last:
+                nc.vector.tensor_copy(picked[:], pages[s][:].indirect(idx3[:]))
             else:
-                nc.vector.tensor_copy(o, i)
+                for hf in range(2):
+                    nc.vector.tensor_copy(
+                        picked[:, half * hf : half * (hf + 1)], pages[s][:].indirect(idx3[:, 16 * hf : 16 * (hf + 1)])
+                    )
+            if s == 2:
+                deal_w4()
+            if s + 2 < SLICES:
+                quantise_w1(s + 2)
+                features(s + 2)
+            if 3 < s + 3 < SLICES:
+                round_w1(s + 3)
+            if 3 < s + 2 < SLICES:
+                weigh(s + 2)
+            if s < 4:
+                for hf in range(2):
+                    turn_rows(pages[s][:, 512 * hf : 512 * (hf + 1)], page_t[:, 4 * hf : 4 * hf + 4, :], s, 2 + hf, F32, ident)
+                size = keep.tile([P, NX], BF16, name="size%d" % s, tag="grouped0" if s == 0 else "size%d" % (s % 2), align_bytes=64)
+                nc.scalar.activation(size[:], picked[:], ACT.Abs, scale=vecs[:, 8 + s : 9 + s])
+                sizes[s] = size
+            elif s < last:
+                for hf in range(2):
+                    round_page(s, hf)
+                for hf in range(2):
+                    size_x(s, hf)
 
-        page_q, x_q = {}, {}
+        xg0 = keep.tile([P, 2 * NX], F32, name="xg0", align_bytes=64)
+        pg0 = keep.tile([P, 2 * T2], F32, name="pg0", align_bytes=64)
+        page_q, x_q, scores = {}, {}, {}
 
-        def quantise_page(k, bank_no, engine):
-            pg = keep.tile([P, 512], F32, name="pg1%d" % k, align_bytes=64)
-            turn_back(page_t[1][k // 2], 2 * (k % 2), pg[:], bank_no, engine)
-            codes = keep.tile([P, 2 * P], U32, name="p_codes1%d" % k, align_bytes=64)
-            scales = keep.tile([P, 2 * P], U8, name="p_scales1%d" % k, align_bytes=64)
-            nc.vector.quantize_mx(out=codes[:].bitcast(FP8X4), scales=scales[:], in_=pg[:].bitcast(BF16))
-            page_q[1, k] = (codes[:], scales[:])
-
-        def score_pass(e, mb, b):
+        def score_pass(mb, b):
             cols = slice(P * (mb % 2), P * (mb % 2 + 1))
             codes, scales = page_q[b, mb // 2]
             nc.tensor.matmul_mx(
-                out=e[:], lhsT=codes[:, cols].bitcast(FP8X4), lhsT_scale=scales[:, cols],
-                rhs=x_q[b][0][:].bitcast(FP8X4), rhs_scale=x_q[b][1][:], start=(b == 0), stop=(b == 1),
+                out=scores[mb][:], lhsT=codes[:, cols].bitcast(FP8X4), lhsT_scale=scales[:, cols],
+                rhs=x_q[b][0].bitcast(FP8X4), rhs_scale=x_q[b][1], start=(b == 0), stop=(b == 1),
             )
 
-        early = {}
-        last = SLICES - 1
         for s in range(SLICES):
             nc.vector.tensor_tensor(pages[s][:].indirect(idx2[:]), feats[s][:], gw[s][:], ALU.mult)
-            if s < last:
-                turn_x(s)
+            if 0 < s < 5:
+                sign_x(s - 1)
+            follow(s)
             if s == 3:
-                xg0 = keep.tile([P, 2 * NX], F32, name="xg0", align_bytes=64)
-                pg0 = keep.tile([P, 2 * T2], F32, name="pg0", align_bytes=64)
+                for k in range(4):
+                    turn_back(page_t, 2 * k, pg0[:, 512 * k : 512 * (k + 1)], 5 + (k + 2) % 3)
+            if s == 4:
                 for k in range(2):
-                    turn_back(x_t[0], 2 * k, xg0[:, 512 * k : 512 * (k + 1)], 5 + k, "scalar")
-            if s in (4, 5):
-                for k in (2 * s - 8, 2 * s - 7):
-                    turn_back(page_t[0][k // 2], 2 * (k % 2), pg0[:, 512 * k : 512 * (k + 1)], 5 + (k + 2) % 3, "scalar")
+                    turn_back(x_t, 2 * k, xg0[:, 512 * k : 512 * (k + 1)], 5 + k)
             if s == 5:
-                codes = keep.tile([P, NX], U32, name="x_codes0", tag="th2", align_bytes=64)
-                scales = keep.tile([P, NX], U8, name="x_scales0", align_bytes=64)
-                nc.vector.quantize_mx(out=codes[:].bitcast(FP8X4), scales=scales[:], in_=xg0[:].bitcast(BF16))
-                x_q[0] = (codes, scales)
-            if s == 6:
-                codes = keep.tile([P, T2], U32, name="p_codes0", tag="gw6", align_bytes=64)
+                codes = keep.tile([P, T2], U32, name="p_codes0", tag="th1", align_bytes=64)
                 scales = keep.tile([P, T2], U8, name="p_scales0", align_bytes=64)
                 nc.vector.quantize_mx(out=codes[:].bitcast(FP8X4), scales=scales[:], in_=pg0[:].bitcast(BF16))
                 for k in range(4):
                     page_q[0, k] = (codes[:, 256 * k : 256 * (k + 1)], scales[:, 256 * k : 256 * (k + 1)])
-        for mb, bank_no in enumerate((7, 0, 1)):
-            early[mb] = bank(bank_no)
-            score_pass(early[mb], mb, 0)
+            if s == 6:
+                codes = keep.tile([P, NX], U32, name="x_codes0", tag="gw6", align_bytes=64)
+                scales = keep.tile([P, NX], U8, name="x_scales0", align_bytes=64)
+                nc.vector.quantize_mx(out=codes[:].bitcast(FP8X4), scales=scales[:], in_=xg0[:].bitcast(BF16))
+                x_q[0] = (codes[:], scales[:])
+                for mb in range(T2 // P):
+                    scores[mb] = bank(mb)
+                    score_pass(mb, 0)
 
-        half = NX // 2
-        picked = [keep.tile([P, half], F32, name="picked7%d" % hf, tag="picked7%d" % hf) for hf in range(2)]
-        size = [keep.tile([P, half], F32, name="size7%d" % hf) for hf in range(2)]
-        xb = [keep.tile([P, half], BF16, name="xb7%d" % hf) for hf in range(2)]
-        for hf in range(2):
-            nc.vector.tensor_copy(picked[hf][:], pages[last][:].indirect(idx3[:, 16 * hf : 16 * (hf + 1)]))
-        turn_page(last, 0, 2)
-        for hf in range(2):
-            nc.scalar.activation(size[hf][:], picked[hf][:], ACT.Abs)
-            nc.vector.tensor_scalar(xb[hf][:], size[hf][:], vecs[:, 8 + last : 9 + last], None, ALU.mult)
-        xg = keep.tile([P, 2 * NX], F32, name="xg1", align_bytes=64)
-        codes = keep.tile([P, NX], U32, name="x_codes1", align_bytes=64)
-        scales = keep.tile([P, NX], U8, name="x_scales1", align_bytes=64)
-        x_q[1] = (codes, scales)
-        for hf in range(2):
-            turn_x_part(last, xb[hf][:], 2 * hf, 2, 4 + hf)
-        for hf in range(2):
-            turn_back(x_t[1], 2 * hf, xg[:, 512 * hf : 512 * (hf + 1)], (6, 4)[hf], ("scalar", "vector")[hf])
-            cols = slice(half * hf, half * (hf + 1))
-            nc.vector.quantize_mx(
-                out=codes[:, cols].bitcast(FP8X4), scales=scales[:, cols], in_=xg[:, 512 * hf : 512 * (hf + 1)].bitcast(BF16)
-            )
-        quantise_page(0, 2, "vector")
-        turn_page(last, 1, 3)
-        quantise_page(1, 5, "scalar")
-        quantise_page(2, 3, "vector")
-        quantise_page(3, 6, "scalar")
-
-        for mb in range(T2 // P):
-            if mb in early:
-                e = early[mb]
+        def weave(planes, name, engine, tag):
+            woven = keep.tile([P, 256, 4], BF16, name=name, tag=tag, align_bytes=64)
+            dst = woven[:].rearrange("p (c i) t -> p c t i", i=8)
+            src = planes.rearrange("p t (c i) -> p c t i", i=8)
+            if engine == "scalar":
+                nc.scalar.copy(dst, src)
             else:
-                e = bank((2, 4, 5, 3, 6)[mb - 3])
-                score_pass(e, mb, 0)
-            score_pass(e, mb, 1)
+                nc.vector.tensor_copy(dst, src)
+            return woven[:].rearrange("p c t -> p (c t)")
+
+        x_codes = keep.tile([P, NX], U32, name="x_codes1", align_bytes=64)
+        x_scales = keep.tile([P, NX], U8, name="x_scales1", align_bytes=64)
+        x_q[1] = (x_codes[:], x_scales[:])
+        woven = {}
+
+        def weave_x(hf, engine):
+            woven["x", hf] = weave(x_planes[hf][:], "woven_x%d" % hf, engine, "woven_x%d" % hf)
+
+        def weave_page(k, engine, tag=None):
+            woven["p", k] = weave(page_planes[k // 2][:, :, 256 * (k % 2) : 256 * (k % 2 + 1)], "woven_p%d" % k, engine, tag or "woven_p%d" % k)
+
+        def quantise_x(hf):
+            cols = slice(half * hf, half * (hf + 1))
+            nc.vector.quantize_mx(out=x_codes[:, cols].bitcast(FP8X4), scales=x_scales[:, cols], in_=woven["x", hf])
+
+        def quantise_page(k):
+            codes = keep.tile([P, 2 * P], U32, name="p_codes1%d" % k, align_bytes=64)
+            scales = keep.tile([P, 2 * P], U8, name="p_scales1%d" % k, align_bytes=64)
+            nc.vector.quantize_mx(out=codes[:].bitcast(FP8X4), scales=scales[:], in_=woven["p", k])
+            page_q[1, k] = (codes[:], scales[:])
+
+        def close_scores(mb, engine):
+            score_pass(mb, 1)
             res = keep.tile([P, NX], F32, name="res%d" % mb, tag="gw%d" % mb if mb < 6 else "res%d" % mb, align_bytes=64)
             bias = vecs[:, 16 + mb : 17 + mb]
-            if mb % 3 != 1:
-                nc.scalar.activation(res[:], e[:], ACT.Identity, bias=bias)
+            if engine == "scalar":
+                nc.scalar.activation(res[:], scores[mb][:], ACT.Identity, bias=bias)
             else:
-                nc.vector.tensor_scalar(res[:], e[:], bias, None, ALU.add)
+                nc.vector.tensor_scalar(res[:], scores[mb][:], bias, None, ALU.add)
             nc.sync.dma_start(out=out[P * mb : P * (mb + 1), :], in_=res[:])
+
+        round_page(last, 0)
+        size_x(last, 0)
+        size_x(last, 1)
+        weave_x(0, "vector")
+        weave_x(1, "vector")
+        round_page(last, 1)
+        weave_page(0, "vector")
+        quantise_page(0)
+        quantise_x(0)
+        quantise_x(1)
+        weave_page(1, "scalar")
+        weave_page(2, "scalar")
+        quantise_page(1)
+        close_scores(0, "scalar")
+        close_scores(1, "scalar")
+        weave_page(3, "vector", "woven_x0")
+        quantise_page(2)
+        quantise_page(3)
+        close_scores(2, "scalar")
+        close_scores(3, "vector")
+        close_scores(4, "scalar")
+        close_scores(5, "vector")
+        close_scores(6, "scalar")
+        close_scores(7, "vector")

@@ -20,7 +20,7 @@ ALU = mybir.AluOpType
 P = 128
 SLICES = H // P
 AHEAD = 3
-PIECES = (1, 1, 1, 4, 2, 2, 2, 8)
+PIECES = (1, 1, 1, 4, 4, 4, 4, 8)
 
 
 def tile_list_linen_wear_register_kernel(
@@ -96,6 +96,7 @@ def tile_list_linen_wear_register_kernel(
                     out=w4_sc[b][32 * q : 32 * q + 4, :, :].bitcast(I32), in_=src.rearrange("a r n -> r a n").bitcast(I32)
                 )
 
+        load_w4_scales(0, nc.gpsimd)
         ident_bf = keep.tile([P, P], BF16, name="ident_bf")
         make_identity(nc, ident_bf[:])
 
@@ -120,12 +121,11 @@ def tile_list_linen_wear_register_kernel(
         move_plane(2)
         load_tab(3)
         load_w4(0)
-        load_w4_scales(0, nc.sync)
+        move_plane(3)
         load_tab(1)
         nc.sync.dma_start(out=wgs_t[:], in_=wgs)
-        move_plane(3)
-        load_page(0, 1)
         nc.sync.dma_start(idx2[:], offs2)
+        load_page(0, 1)
         nc.sync.dma_start(idx3[:], offs3)
         load_w1(1, 256, 512, 2)
         for r0, vec in ((4, gain), (12, rv)):
@@ -136,8 +136,8 @@ def tile_list_linen_wear_register_kernel(
         nc.sync.dma_start(out=rows[1][8:12, :], in_=rv[0:512].rearrange("(s p) -> s p", p=P))
         nc.sync.dma_start(out=rows[1][16:24, :], in_=slot.rearrange("(s p) -> s p", p=P))
         load_page(1, PIECES[1])
-        load_w1(2, 512, H, 4)
         load_w4(1)
+        load_w1(2, 512, H, 4)
         load_w4_scales(1, nc.sync)
         load_page(2, PIECES[2])
         load_wgs_dealt(0)
@@ -149,7 +149,13 @@ def tile_list_linen_wear_register_kernel(
 
         v = [keep.tile([P, S], U32, name="v%d" % a, align_bytes=64) for a in range(4)]
         for a in (0, 2, 3, 1):
-            nc.vector.tensor_copy(v[a][:], tab[a][:].indirect(idx[:]))
+            if a != 1:
+                nc.vector.tensor_copy(v[a][:], tab[a][:].indirect(idx[:]))
+            else:
+                for hf in range(2):
+                    nc.vector.tensor_copy(
+                        v[a][:, 256 * hf : 256 * (hf + 1)], tab[a][:].indirect(idx[:, 16 * hf : 16 * (hf + 1)])
+                    )
         v_plane = [v_sc[:, :], v_sc[4:P, :], v_sc23[:, 0, :], v_sc23[:, 1, :]]
 
         first_gains = keep.tile([P, 4], F32, name="first_gains")
@@ -204,20 +210,28 @@ def tile_list_linen_wear_register_kernel(
 
         def features(s):
             codes, scales = w1_q[s]
-            f = bank(s % 2)
-            for n, a in enumerate((0, 2, 3, 1) if s == 0 else (2, 3, 0, 1)):
-                if a >= 2:
-                    lhsT = w4[s // 4][:, a - 2, 2 * P * (s % 4) : 2 * P * (s % 4 + 1)].bitcast(FP4X4)
-                    lhsT_scale = w4_sc[s // 4][:, a - 2, P * (s % 4) : P * (s % 4 + 1)]
-                else:
-                    lhsT = codes[:, P * a : P * (a + 1)].bitcast(FP8X4)
-                    lhsT_scale = scales[:, P * a : P * (a + 1)]
-                nc.tensor.matmul_mx(
-                    out=f[:], lhsT=lhsT, lhsT_scale=lhsT_scale, rhs=v[a][:].bitcast(FP8X4), rhs_scale=v_plane[a],
-                    start=(n == 0), stop=(n == 3),
-                )
             th = keep.tile([P, S], F32, name="th%d" % s, tag="th%d" % (s % 4), align_bytes=64)
-            nc.scalar.activation(th[:], f[:], ACT.Tanh)
+            if s == 0:
+                parts, order = ((0, 0, 256), (2, 256, 512)), (0, 2, 3, 1)
+            else:
+                parts, order = ((s % 2, 0, 512),), (2, 3, 0, 1)
+            for bank_no, j0, j1 in parts:
+                f = bank(bank_no)
+                for a in order:
+                    if a >= 2:
+                        lhsT = w4[s // 4][:, a - 2, 2 * P * (s % 4) : 2 * P * (s % 4 + 1)].bitcast(FP4X4)
+                        lhsT_scale = w4_sc[s // 4][:, a - 2, P * (s % 4) : P * (s % 4 + 1)]
+                    else:
+                        lhsT = codes[:, P * a : P * (a + 1)].bitcast(FP8X4)
+                        lhsT_scale = scales[:, P * a : P * (a + 1)]
+                    width = P if a >= 2 and s == 0 else j1 - j0
+                    for j in range(j0, j1, width):
+                        nc.tensor.matmul_mx(
+                            out=f[:, j - j0 : j - j0 + width], lhsT=lhsT, lhsT_scale=lhsT_scale,
+                            rhs=v[a][:, j : j + width].bitcast(FP8X4), rhs_scale=v_plane[a][:, j : j + width],
+                            start=(a == order[0]), stop=(a == order[-1]),
+                        )
+                nc.scalar.activation(th[:, j0:j1], f[:, 0 : j1 - j0], ACT.Tanh)
             feats[s] = th
 
         gw = {}
@@ -261,6 +275,8 @@ def tile_list_linen_wear_register_kernel(
 
         page_planes = [keep.tile([P, 4, T2 // 2], BF16, name="page_planes%d" % hf) for hf in range(2)]
         x_planes = [keep.tile([P, 4, NX // 2], BF16, name="x_planes%d" % hf) for hf in range(2)]
+        for planes in page_planes[:1] + x_planes:
+            nc.gpsimd.memset(planes[:, 3, :], 0.0)
         sizes = {}
         last = SLICES - 1
         half = NX // 2
@@ -271,6 +287,32 @@ def tile_list_linen_wear_register_kernel(
             turn_rows(xb[:], x_t[:], s, 4, BF16, ident_bf)
 
         picks = {}
+        woven_page = [keep.tile([P, 256, 4], BF16, name="woven_p%d" % k, align_bytes=64) for k in range(4)]
+        woven_x = [keep.tile([P, 256, 4], BF16, name="woven_x%d" % hf, align_bytes=64) for hf in range(2)]
+
+        def weave(woven, planes, engine="scalar"):
+            dst = woven[:].rearrange("p (c i) t -> p c t i", i=4)
+            src = planes.rearrange("p t (c i) -> p c t i", i=4)
+            if engine == "scalar":
+                nc.scalar.copy(dst, src)
+            else:
+                nc.vector.tensor_copy(dst, src)
+
+        def weave_page(k, engine="scalar"):
+            weave(woven_page[k], page_planes[k // 2][:, :, 256 * (k % 2) : 256 * (k % 2 + 1)], engine)
+
+        def weave_x(hf):
+            weave(woven_x[hf], x_planes[hf][:])
+
+        def last_page(k):
+            nc.vector.tensor_scalar(
+                woven_page[k][:, :, 3], pages[last][:, 256 * k : 256 * (k + 1)], signs[:, last : last + 1], None, ALU.mult
+            )
+
+        def last_x(hf):
+            nc.scalar.activation(
+                woven_x[hf][:, :, 3], picks[last][:, half * hf : half * (hf + 1)], ACT.Abs, scale=vecs[:, 8 + last : 9 + last]
+            )
 
         def round_page(s, hf):
             nc.scalar.activation(
@@ -310,6 +352,8 @@ def tile_list_linen_wear_register_kernel(
             elif s < last:
                 for hf in range(2):
                     round_page(s, hf)
+                if s == last - 1:
+                    weave_page(0)
                 for hf in range(2):
                     size_x(s, hf)
 
@@ -326,7 +370,10 @@ def tile_list_linen_wear_register_kernel(
             )
 
         for s in range(SLICES):
-            nc.vector.tensor_tensor(pages[s][:].indirect(idx2[:]), feats[s][:], gw[s][:], ALU.mult)
+            for j0, j1 in ((0, 256), (256, 512)) if s == 0 else ((0, 512),):
+                nc.vector.tensor_tensor(
+                    pages[s][:].indirect(idx2[:, j0 // 16 : j1 // 16]), feats[s][:, j0:j1], gw[s][:, j0:j1], ALU.mult
+                )
             if 0 < s < 5:
                 sign_x(s - 1)
             follow(s)
@@ -343,6 +390,9 @@ def tile_list_linen_wear_register_kernel(
                 for k in range(4):
                     page_q[0, k] = (codes[:, 256 * k : 256 * (k + 1)], scales[:, 256 * k : 256 * (k + 1)])
             if s == 6:
+                for hf in range(2):
+                    weave_x(hf)
+                weave_page(1)
                 codes = keep.tile([P, NX], U32, name="x_codes0", tag="gw6", align_bytes=64)
                 scales = keep.tile([P, NX], U8, name="x_scales0", align_bytes=64)
                 nc.vector.quantize_mx(out=codes[:].bitcast(FP8X4), scales=scales[:], in_=xg0[:].bitcast(BF16))
@@ -351,35 +401,17 @@ def tile_list_linen_wear_register_kernel(
                     scores[mb] = bank(mb)
                     score_pass(mb, 0)
 
-        def weave(planes, name, engine, tag):
-            woven = keep.tile([P, 256, 4], BF16, name=name, tag=tag, align_bytes=64)
-            dst = woven[:].rearrange("p (c i) t -> p c t i", i=8)
-            src = planes.rearrange("p t (c i) -> p c t i", i=8)
-            if engine == "scalar":
-                nc.scalar.copy(dst, src)
-            else:
-                nc.vector.tensor_copy(dst, src)
-            return woven[:].rearrange("p c t -> p (c t)")
-
         x_codes = keep.tile([P, NX], U32, name="x_codes1", align_bytes=64)
         x_scales = keep.tile([P, NX], U8, name="x_scales1", align_bytes=64)
         x_q[1] = (x_codes[:], x_scales[:])
-        woven = {}
-
-        def weave_x(hf, engine):
-            woven["x", hf] = weave(x_planes[hf][:], "woven_x%d" % hf, engine, "woven_x%d" % hf)
-
-        def weave_page(k, engine, tag=None):
-            woven["p", k] = weave(page_planes[k // 2][:, :, 256 * (k % 2) : 256 * (k % 2 + 1)], "woven_p%d" % k, engine, tag or "woven_p%d" % k)
-
         def quantise_x(hf):
             cols = slice(half * hf, half * (hf + 1))
-            nc.vector.quantize_mx(out=x_codes[:, cols].bitcast(FP8X4), scales=x_scales[:, cols], in_=woven["x", hf])
+            nc.vector.quantize_mx(out=x_codes[:, cols].bitcast(FP8X4), scales=x_scales[:, cols], in_=woven_x[hf][:].rearrange("p c t -> p (c t)"))
 
         def quantise_page(k):
             codes = keep.tile([P, 2 * P], U32, name="p_codes1%d" % k, align_bytes=64)
             scales = keep.tile([P, 2 * P], U8, name="p_scales1%d" % k, align_bytes=64)
-            nc.vector.quantize_mx(out=codes[:].bitcast(FP8X4), scales=scales[:], in_=woven["p", k])
+            nc.vector.quantize_mx(out=codes[:].bitcast(FP8X4), scales=scales[:], in_=woven_page[k][:].rearrange("p c t -> p (c t)"))
             page_q[1, k] = (codes[:], scales[:])
 
         def close_scores(mb, engine):
@@ -392,27 +424,24 @@ def tile_list_linen_wear_register_kernel(
                 nc.vector.tensor_scalar(res[:], scores[mb][:], bias, None, ALU.add)
             nc.sync.dma_start(out=out[P * mb : P * (mb + 1), :], in_=res[:])
 
-        round_page(last, 0)
-        size_x(last, 0)
-        size_x(last, 1)
-        weave_x(0, "vector")
-        weave_x(1, "vector")
-        round_page(last, 1)
-        weave_page(0, "vector")
+        last_x(0)
+        last_x(1)
+        last_page(0)
+        last_page(1)
         quantise_page(0)
         quantise_x(0)
         quantise_x(1)
-        weave_page(1, "scalar")
-        weave_page(2, "scalar")
         quantise_page(1)
+        round_page(last, 1)
+        weave_page(2, "vector")
         close_scores(0, "scalar")
-        close_scores(1, "scalar")
-        weave_page(3, "vector", "woven_x0")
         quantise_page(2)
-        quantise_page(3)
+        close_scores(1, "scalar")
+        weave_page(3, "vector")
         close_scores(2, "scalar")
-        close_scores(3, "vector")
-        close_scores(4, "scalar")
-        close_scores(5, "vector")
-        close_scores(6, "scalar")
-        close_scores(7, "vector")
+        quantise_page(3)
+        close_scores(3, "scalar")
+        close_scores(4, "vector")
+        close_scores(5, "scalar")
+        close_scores(6, "vector")
+        close_scores(7, "scalar")

from contextlib import ExitStack

import concourse.mybir as mybir
from concourse.masks import make_identity

K, K1, H, T, S, T2, NX = 2048, 1024, 1024, 2048, 512, 1024, 512
FLOPS = 2 * K * H * S + 2 * H * T2 * NX

F32 = mybir.dt.float32
BF16 = mybir.dt.bfloat16
I32 = mybir.dt.int32
U32 = mybir.dt.uint32
U16 = mybir.dt.uint16
U8 = mybir.dt.uint8
FP8X4 = mybir.dt.float8_e4m3fn_x4
FP4X4 = mybir.dt.float4_e2m1fn_x4
ACT = mybir.ActivationFunctionType
ALU = mybir.AluOpType

P = 128
SLICES = H // P
AHEAD = 3
PIECES = (1, 1, 1, 4, 4, 4, 4, 8)


def tile_list_linen_wear_register_kernel(
    tc, tab_words, tab_scales, offs, w1, w4_words, w4_scales, gain, page0, wgs, offs2, offs3, rv, slot, out
):
    nc = tc.nc
    with ExitStack() as ctx:
        keep = ctx.enter_context(tc.tile_pool(name="keep", bufs=1))
        psum = ctx.enter_context(tc.psum_pool(name="psum", bufs=1))

        def bank(i, dtype=F32):
            return psum.tile([P, 512], dtype, name="bank%d" % i, tag="bank%d" % i)

        idx = keep.tile([P, S // 16], U16, name="idx")
        idx2 = keep.tile([P, S // 16], U16, name="idx2")
        idx3 = keep.tile([P, NX // 16], U16, name="idx3")

        tab = [keep.tile([P, T], U32, name="tab%d" % a, align_bytes=64) for a in range(4)]
        tab_sc = keep.tile([P, T], U8, name="tab_sc", align_bytes=64)
        v_sc23 = keep.tile([P, 2, S], U8, name="v_sc23", align_bytes=64)
        w4 = [keep.tile([P, 2, H], U8, name="w4_%d" % b, align_bytes=64) for b in range(2)]
        w4_sc = [keep.tile([P, 2, H // 2], U8, name="w4_sc%d" % b, align_bytes=64) for b in range(2)]
        rows = [keep.tile([P, P], F32, name="rows%d" % i) for i in range(2)]
        wgs_t = keep.tile([P, S], F32, name="wgs_t")
        pages = [keep.tile([P, T2], F32, name="page%d" % s) for s in range(SLICES)]
        w1_raw = [keep.tile([P, 2, 4, 2 * P], F32, name="w1_raw%d" % d, tag="w1_raw%d" % d) for d in range(2)]
        w1_raw.append(keep.tile([P, 2, 4, 4 * P], F32, name="w1_raw2"))
        wgs_dealt = [keep.tile([P, S], F32, name="wgs_dealt%d" % t) for t in range(4)]

        nc.gpsimd.memset(tab_sc[:, 0 : T // 2].bitcast(I32), 0)
        nc.vector.memset(tab_sc[:, T // 2 : T].bitcast(I32), 0)
        nc.vector.memset(v_sc23[:].rearrange("p a n -> p (a n)").bitcast(I32), 0)
        for i in range(2):
            nc.gpsimd.memset(rows[i][:], 0.0)
        for b in range(2):
            nc.vector.memset(w4_sc[b][:].rearrange("p a n -> p (a n)").bitcast(I32), 0)
        nc.gpsimd.dma_start(out=rows[0][0:4, :], in_=gain[0:512].rearrange("(s p) -> s p", p=P))
        ident = keep.tile([P, P], F32, name="ident")
        make_identity(nc, ident[:])

        def load_tab(a):
            nc.sync.dma_start(out=tab[a][:].bitcast(I32), in_=tab_words[a].rearrange("p t i -> p (t i)").bitcast(I32))

        def load_w1(d, c0, c1, pieces):
            rows_a_piece = 8 // pieces
            for a in range(2):
                src = w1[512 * a : 512 * (a + 1), c0:c1].rearrange("(p j) c -> p j c", j=4)
                for j in range(0, 4, rows_a_piece):
                    nc.sync.dma_start(out=w1_raw[d][:, a, j : j + rows_a_piece, :], in_=src[:, j : j + rows_a_piece, :])

        def load_page(s, pieces):
            width = T2 // pieces
            for c in range(0, T2, width):
                if s < 4:
                    src = page0[P * s : P * (s + 1), c : c + width]
                else:
                    src = page0[512:H, c : c + width].rearrange("(g t i) m -> t g i m", t=4, i=8)[s - 4]
                nc.sync.dma_start(out=pages[s][:, c : c + width], in_=src)

        def load_wgs_dealt(t):
            for q in range(4):
                src = wgs.rearrange("(g t i) j -> t g i j", t=4, i=8)[t]
                nc.sync.dma_start(out=wgs_dealt[t][32 * q : 32 * (q + 1), :], in_=src)

        def load_w4(b):
            src = w4_words[:, :, H * b : H * (b + 1)]
            nc.sync.dma_start(out=w4[b][:].bitcast(I32), in_=src.rearrange("a p n -> p a n").bitcast(I32))

        def load_w4_scales(b, queue):
            for q in range(4):
                src = w4_scales[:, 4 * q : 4 * q + 4, 512 * b : 512 * (b + 1)]
                queue.dma_start(
                    out=w4_sc[b][32 * q : 32 * q + 4, :, :].bitcast(I32), in_=src.rearrange("a r n -> r a n").bitcast(I32)
                )

        load_w4_scales(0, nc.gpsimd)
        ident_bf = keep.tile([P, P], BF16, name="ident_bf")
        make_identity(nc, ident_bf[:])

        v_sc = keep.tile([P, S], U8, name="v_sc", align_bytes=64)

        def move_plane(a):
            for q in range(4):
                nc.sync.dma_start(
                    out=v_sc23[32 * q : 32 * q + 4, a - 2, :].bitcast(I32),
                    in_=v_sc[32 * q + 4 * a : 32 * q + 4 * a + 4, :].bitcast(I32),
                )

        load_tab(0)
        nc.sync.dma_start(idx[:], offs)
        for q in range(4):
            nc.sync.dma_start(
                out=tab_sc[32 * q : 32 * q + 16, :].bitcast(I32), in_=tab_scales[:, 4 * q : 4 * q + 4, :].bitcast(I32)
            )
        nc.vector.tensor_copy(v_sc[:], tab_sc[:].indirect(idx[:]))
        load_tab(2)
        load_w1(0, 0, 256, 2)
        move_plane(2)
        load_tab(3)
        load_w4(0)
        move_plane(3)
        load_tab(1)
        nc.sync.dma_start(out=wgs_t[:], in_=wgs)
        nc.sync.dma_start(idx2[:], offs2)
        load_page(0, 1)
        nc.sync.dma_start(idx3[:], offs3)
        load_w1(1, 256, 512, 2)
        for r0, vec in ((4, gain), (12, rv)):
            nc.sync.dma_start(
                out=rows[1][r0 : r0 + 4, :].rearrange("t (g i) -> t g i", i=8),
                in_=vec[512:H].rearrange("(g t i) -> t g i", t=4, i=8),
            )
        nc.sync.dma_start(out=rows[1][8:12, :], in_=rv[0:512].rearrange("(s p) -> s p", p=P))
        nc.sync.dma_start(out=rows[1][16:24, :], in_=slot.rearrange("(s p) -> s p", p=P))
        load_page(1, PIECES[1])
        load_w4(1)
        load_w1(2, 512, H, 4)
        load_w4_scales(1, nc.sync)
        load_page(2, PIECES[2])
        load_wgs_dealt(0)
        load_page(3, PIECES[3])
        for s in range(4, SLICES):
            if s < SLICES - 1:
                load_wgs_dealt(s - 3)
            load_page(s, PIECES[s])

        v = [keep.tile([P, S], U32, name="v%d" % a, align_bytes=64) for a in range(4)]
        for a in (0, 2, 3, 1):
            if a != 1:
                nc.vector.tensor_copy(v[a][:], tab[a][:].indirect(idx[:]))
            else:
                for hf in range(2):
                    nc.vector.tensor_copy(
                        v[a][:, 256 * hf : 256 * (hf + 1)], tab[a][:].indirect(idx[:, 16 * hf : 16 * (hf + 1)])
                    )
        v_plane = [v_sc[:, :], v_sc[4:P, :], v_sc23[:, 0, :], v_sc23[:, 1, :]]

        first_gains = keep.tile([P, 4], F32, name="first_gains")
        vecs = keep.tile([P, 24], F32, name="vecs")
        for i, dst in enumerate((first_gains, vecs)):
            turned = bank(7 - i)
            nc.tensor.transpose(turned[:, 0:P], rows[i][:], ident[:])
            nc.scalar.copy(dst[:], turned[:, 0 : (4, 24)[i]])
        signs = keep.tile([P, SLICES], F32, name="signs")
        halves = keep.tile([P, SLICES], F32, name="halves")
        nc.gpsimd.tensor_scalar(halves[:], vecs[:, 8:16], 0.0, 0.5, ALU.is_ge, ALU.subtract)
        nc.gpsimd.tensor_scalar(signs[:], halves[:], 2.0, 0.0, ALU.mult, ALU.add)

        w1_q = {}

        w1_bf = {}

        def round_w1(s):
            slot_name = "grouped%d" % (s % 2)
            grouped = keep.tile([P, 2, P, 4], BF16, name="w1_grouped%d" % s, tag=slot_name, align_bytes=64)
            if s < 4:
                nc.scalar.copy(
                    grouped[:].rearrange("p a (c i) j -> p a c j i", i=4),
                    w1_raw[s // 2][:, :, :, P * (s % 2) : P * (s % 2 + 1)].rearrange("p a j (c i) -> p a c j i", i=4),
                )
            else:
                nc.scalar.copy(
                    grouped[:].rearrange("p a (g i) j -> p a g j i", i=8),
                    w1_raw[2][:].rearrange("p a j (g t i) -> p t a g j i", t=4, i=8)[:, s - 4],
                )
            w1_bf[s] = grouped

        def quantise_w1(s):
            codes = keep.tile([P, 2 * P], U32, name="w1_codes%d" % s, tag="gw%d" % (s - 2 if s > 1 else 1 + 2 * s), align_bytes=64)
            scales = keep.tile([P, 2 * P], U8, name="w1_scales%d" % s, tag="gw2" if s == 0 else "w1_scales%d" % s, align_bytes=64)
            nc.vector.quantize_mx(
                out=codes[:].bitcast(FP8X4), scales=scales[:], in_=w1_bf[s][:].rearrange("p a c j -> p (a c j)")
            )
            w1_q[s] = (codes, scales)

        feats = {}

        def deal_w4():
            words = keep.tile([P, 2, H], U8, name="w4_dealt", align_bytes=64)
            scales = keep.tile([P, 2, H // 2], U8, name="w4_sc_dealt", align_bytes=64)
            for dst, src, w in ((words, w4[1], 4), (scales, w4_sc[1], 2)):
                nc.vector.tensor_copy(
                    dst[:].bitcast(I32).rearrange("p a (t g w) -> p a t g w", t=4, w=w),
                    src[:].bitcast(I32).rearrange("p a (g t w) -> p a t g w", t=4, w=w),
                )
            w4[1], w4_sc[1] = words, scales

        def features(s):
            codes, scales = w1_q[s]
            th = keep.tile([P, S], F32, name="th%d" % s, tag="th%d" % (s % 4), align_bytes=64)
            if s == 0:
                parts, order = ((0, 0, 256), (2, 256, 512)), (0, 2, 3, 1)
            else:
                parts, order = ((s % 2, 0, 512),), (2, 3, 0, 1)
            for bank_no, j0, j1 in parts:
                f = bank(bank_no)
                for a in order:
                    if a >= 2:
                        lhsT = w4[s // 4][:, a - 2, 2 * P * (s % 4) : 2 * P * (s % 4 + 1)].bitcast(FP4X4)
                        lhsT_scale = w4_sc[s // 4][:, a - 2, P * (s % 4) : P * (s % 4 + 1)]
                    else:
                        lhsT = codes[:, P * a : P * (a + 1)].bitcast(FP8X4)
                        lhsT_scale = scales[:, P * a : P * (a + 1)]
                    width = P if a >= 2 and s == 0 else j1 - j0
                    for j in range(j0, j1, width):
                        nc.tensor.matmul_mx(
                            out=f[:, j - j0 : j - j0 + width], lhsT=lhsT, lhsT_scale=lhsT_scale,
                            rhs=v[a][:, j : j + width].bitcast(FP8X4), rhs_scale=v_plane[a][:, j : j + width],
                            start=(a == order[0]), stop=(a == order[-1]),
                        )
                nc.scalar.activation(th[:, j0:j1], f[:, 0 : j1 - j0], ACT.Tanh)
            feats[s] = th

        gw = {}

        def weigh(s):
            src, gains = (wgs_t, first_gains) if s < 4 else (wgs_dealt[s - 4], vecs)
            gw[s] = keep.tile([P, S], F32, name="gw%d" % s, tag="gw%d" % s, align_bytes=64)
            nc.scalar.activation(gw[s][:], src[:], ACT.Copy, scale=gains[:, s : s + 1])

        for s in range(2):
            round_w1(s)
            quantise_w1(s)
        for s in range(2):
            features(s)
            weigh(s)
        for s in range(2, 4):
            round_w1(s)
        for s in range(2, 4):
            weigh(s)

        page_t = keep.tile([P, 8, 512], BF16, name="page_t0", tag="w1_raw1")
        x_t = keep.tile([P, 4, 512], BF16, name="x_t0")

        def laid(dst, q):
            return dst.rearrange("p c (u g i) -> p c g u i", u=2, i=16)[:, :, 4 * q : 4 * q + 4, :, :]

        def turn_rows(src, dst, q, bank_no, dtype, identity):
            turned_rows = bank(bank_no, dtype)
            for c in range(4):
                nc.tensor.transpose(turned_rows[:, P * c : P * (c + 1)], src[:, P * c : P * (c + 1)], identity[:])
            nc.scalar.copy(laid(dst, q), turned_rows[:].rearrange("p (c g u i) -> p c g u i", c=4, u=2, i=16))

        def turn_back(src, c0, dst, bank_no):
            words = src[:].rearrange("p c n -> p (c n)").bitcast(F32)
            back = bank(bank_no)
            for c in range(2):
                for u in range(2):
                    w0 = 256 * (c0 + c) + P * u
                    nc.tensor.transpose(back[:, P * (2 * c + u) : P * (2 * c + u + 1)], words[:, w0 : w0 + P], ident[:])
            nc.scalar.copy(dst.rearrange("p (c m u) -> p c m u", c=2, u=2), back[:].rearrange("p (c u m) -> p c m u", c=2, u=2))

        page_planes = [keep.tile([P, 4, T2 // 2], BF16, name="page_planes%d" % hf) for hf in range(2)]
        x_planes = [keep.tile([P, 4, NX // 2], BF16, name="x_planes%d" % hf) for hf in range(2)]
        for planes in page_planes[:1] + x_planes:
            nc.gpsimd.memset(planes[:, 3, :], 0.0)
        sizes = {}
        last = SLICES - 1
        half = NX // 2

        def sign_x(s):
            xb = keep.tile([P, NX], BF16, name="xb%d" % s, tag="th%d" % ((s + 1) % 4), align_bytes=64)
            nc.vector.tensor_scalar(xb[:], sizes[s][:], signs[:, s : s + 1], None, ALU.mult)
            turn_rows(xb[:], x_t[:], s, 4, BF16, ident_bf)

        picks = {}
        woven_page = [keep.tile([P, 256, 4], BF16, name="woven_p%d" % k, align_bytes=64) for k in range(4)]
        woven_x = [keep.tile([P, 256, 4], BF16, name="woven_x%d" % hf, align_bytes=64) for hf in range(2)]

        def weave(woven, planes, engine="scalar"):
            dst = woven[:].rearrange("p (c i) t -> p c t i", i=4)
            src = planes.rearrange("p t (c i) -> p c t i", i=4)
            if engine == "scalar":
                nc.scalar.copy(dst, src)
            else:
                nc.vector.tensor_copy(dst, src)

        def weave_page(k, engine="scalar"):
            weave(woven_page[k], page_planes[k // 2][:, :, 256 * (k % 2) : 256 * (k % 2 + 1)], engine)

        def weave_x(hf):
            weave(woven_x[hf], x_planes[hf][:])

        def last_page(k):
            nc.vector.tensor_scalar(
                woven_page[k][:, :, 3], pages[last][:, 256 * k : 256 * (k + 1)], signs[:, last : last + 1], None, ALU.mult
            )

        def last_x(hf):
            nc.scalar.activation(
                woven_x[hf][:, :, 3], picks[last][:, half * hf : half * (hf + 1)], ACT.Abs, scale=vecs[:, 8 + last : 9 + last]
            )

        def round_page(s, hf):
            nc.scalar.activation(
                page_planes[hf][:, s - 4, :], pages[s][:, 512 * hf : 512 * (hf + 1)], ACT.Copy, scale=signs[:, s : s + 1]
            )

        def size_x(s, hf):
            nc.scalar.activation(
                x_planes[hf][:, s - 4, :], picks[s][:, half * hf : half * (hf + 1)], ACT.Abs, scale=vecs[:, 8 + s : 9 + s]
            )

        def follow(s):
            picked = keep.tile([P, NX], F32, name="picked%d" % s, tag="picked%d" % (s % 2), align_bytes=64)
            picks[s] = picked
            if s < last:
                nc.vector.tensor_copy(picked[:], pages[s][:].indirect(idx3[:]))
            else:
                for hf in range(2):
                    nc.vector.tensor_copy(
                        picked[:, half * hf : half * (hf + 1)], pages[s][:].indirect(idx3[:, 16 * hf : 16 * (hf + 1)])
                    )
            if s == 2:
                deal_w4()
            if s + 2 < SLICES:
                quantise_w1(s + 2)
                features(s + 2)
            if 3 < s + 3 < SLICES:
                round_w1(s + 3)
            if 3 < s + 2 < SLICES:
                weigh(s + 2)
            if s < 4:
                for hf in range(2):
                    turn_rows(pages[s][:, 512 * hf : 512 * (hf + 1)], page_t[:, 4 * hf : 4 * hf + 4, :], s, 2 + hf, F32, ident)
                size = keep.tile([P, NX], BF16, name="size%d" % s, tag="grouped0" if s == 0 else "size%d" % (s % 2), align_bytes=64)
                nc.scalar.activation(size[:], picked[:], ACT.Abs, scale=vecs[:, 8 + s : 9 + s])
                sizes[s] = size
            elif s < last:
                for hf in range(2):
                    round_page(s, hf)
                if s == last - 1:
                    weave_page(0)
                for hf in range(2):
                    size_x(s, hf)

        xg0 = keep.tile([P, 2 * NX], F32, name="xg0", align_bytes=64)
        pg0 = keep.tile([P, 2 * T2], F32, name="pg0", align_bytes=64)
        page_q, x_q, scores = {}, {}, {}

        def score_pass(mb, b):
            cols = slice(P * (mb % 2), P * (mb % 2 + 1))
            codes, scales = page_q[b, mb // 2]
            nc.tensor.matmul_mx(
                out=scores[mb][:], lhsT=codes[:, cols].bitcast(FP8X4), lhsT_scale=scales[:, cols],
                rhs=x_q[b][0].bitcast(FP8X4), rhs_scale=x_q[b][1], start=(b == 0), stop=(b == 1),
            )

        for s in range(SLICES):
            for j0, j1 in ((0, 256), (256, 512)) if s == 0 else ((0, 512),):
                nc.vector.tensor_tensor(
                    pages[s][:].indirect(idx2[:, j0 // 16 : j1 // 16]), feats[s][:, j0:j1], gw[s][:, j0:j1], ALU.mult
                )
            if 0 < s < 5:
                sign_x(s - 1)
            follow(s)
            if s == 3:
                for k in range(4):
                    turn_back(page_t, 2 * k, pg0[:, 512 * k : 512 * (k + 1)], 5 + (k + 2) % 3)
            if s == 4:
                for k in range(2):
                    turn_back(x_t, 2 * k, xg0[:, 512 * k : 512 * (k + 1)], 5 + k)
            if s == 5:
                codes = keep.tile([P, T2], U32, name="p_codes0", tag="th1", align_bytes=64)
                scales = keep.tile([P, T2], U8, name="p_scales0", align_bytes=64)
                nc.vector.quantize_mx(out=codes[:].bitcast(FP8X4), scales=scales[:], in_=pg0[:].bitcast(BF16))
                for k in range(4):
                    page_q[0, k] = (codes[:, 256 * k : 256 * (k + 1)], scales[:, 256 * k : 256 * (k + 1)])
            if s == 6:
                for hf in range(2):
                    weave_x(hf)
                weave_page(1)
                codes = keep.tile([P, NX], U32, name="x_codes0", tag="gw6", align_bytes=64)
                scales = keep.tile([P, NX], U8, name="x_scales0", align_bytes=64)
                nc.vector.quantize_mx(out=codes[:].bitcast(FP8X4), scales=scales[:], in_=xg0[:].bitcast(BF16))
                x_q[0] = (codes[:], scales[:])
                for mb in range(T2 // P):
                    scores[mb] = bank(mb)
                    score_pass(mb, 0)

        x_codes = keep.tile([P, NX], U32, name="x_codes1", align_bytes=64)
        x_scales = keep.tile([P, NX], U8, name="x_scales1", align_bytes=64)
        x_q[1] = (x_codes[:], x_scales[:])
        def quantise_x(hf):
            cols = slice(half * hf, half * (hf + 1))
            nc.vector.quantize_mx(out=x_codes[:, cols].bitcast(FP8X4), scales=x_scales[:, cols], in_=woven_x[hf][:].rearrange("p c t -> p (c t)"))

        def quantise_page(k):
            codes = keep.tile([P, 2 * P], U32, name="p_codes1%d" % k, align_bytes=64)
            scales = keep.tile([P, 2 * P], U8, name="p_scales1%d" % k, align_bytes=64)
            nc.vector.quantize_mx(out=codes[:].bitcast(FP8X4), scales=scales[:], in_=woven_page[k][:].rearrange("p c t -> p (c t)"))
            page_q[1, k] = (codes[:], scales[:])

        def close_scores(mb, engine):
            score_pass(mb, 1)
            res = keep.tile([P, NX], F32, name="res%d" % mb, tag="gw%d" % mb if mb < 6 else "res%d" % mb, align_bytes=64)
            bias = vecs[:, 16 + mb : 17 + mb]
            if engine == "scalar":
                nc.scalar.activation(res[:], scores[mb][:], ACT.Identity, bias=bias)
            else:
                nc.vector.tensor_scalar(res[:], scores[mb][:], bias, None, ALU.add)
            nc.sync.dma_start(out=out[P * mb : P * (mb + 1), :], in_=res[:])

        last_x(0)
        last_x(1)
        last_page(0)
        last_page(1)
        quantise_page(0)
        quantise_x(0)
        quantise_x(1)
        quantise_page(1)
        round_page(last, 1)
        weave_page(2, "vector")
        close_scores(0, "scalar")
        quantise_page(2)
        close_scores(1, "scalar")
        weave_page(3, "vector")
        close_scores(2, "scalar")
        quantise_page(3)
        close_scores(3, "scalar")
        close_scores(4, "vector")
        close_scores(5, "scalar")
        close_scores(6, "vector")
        close_scores(7, "scalar")
